import numpy as np, ml_dtypes
CORES = [9,25,41,57]
N = 4
import mx_ref
BF = ml_dtypes.bfloat16
def gentries(a):
    return np.ascontiguousarray(a.reshape(8, 16, -1).transpose(0, 2, 1)).reshape(8, -1)
def gtable(e):
    e = np.asarray(e); return np.ascontiguousarray(e.reshape(8, -1, 16).transpose(0, 2, 1)).reshape(128, -1).astype(np.int32)
def gcols(t, e):
    v = np.concatenate([t.reshape(8, 16, -1, 4), np.zeros((8, 16, 1, 4), BF)], axis=2)
    return np.ascontiguousarray(np.stack([v[g][:, e[g]] for g in range(8)])).reshape(128, -1)
def tile(rs):
    return np.stack(rs, axis=2).reshape(128, -1).astype(BF)
def cut(t, i, w=512):
    return t[:, w * i:w * i + w]
def pick(q, e):
    c = np.concatenate([q[0].reshape(128, -1, 4), np.zeros((128, 1, 4), np.uint8)], axis=1); s = np.concatenate([q[1], np.ones((16, 1), np.uint8)], axis=1)
    return (np.ascontiguousarray(c[:, e].reshape(128, -1)), np.ascontiguousarray(s[:, e]))
def join(*qs):
    return (np.concatenate([q[0] for q in qs], axis=1), np.concatenate([q[1] for q in qs], axis=1))
def put(q, e, v):
    c, s = q[0].reshape(128, -1, 4).copy(), q[1].copy(); c[:, e] = v[0].reshape(128, -1, 4); s[:, e] = v[1]
    return (c.reshape(128, -1), s)
def pk(c, s):
    return (np.ascontiguousarray(c), mx_ref.live(s))
def emit(q):
    return q[0], q[1]
def packed(v, rng):
    q = [mx_ref.quantize(np.ascontiguousarray(v[r])) for r in range(N)]
    return np.stack([a for a, b in q]), np.stack([mx_ref.plane(b, rng) for a, b in q])
def values_of_codes():
    e, c = np.zeros((128, 128, 4), np.float32), np.zeros((128, 2, 4), np.uint8)
    e[np.arange(128), np.arange(128), 0] = 1
    c[:127, :, 0] = np.arange(256).reshape(2, 128).T[:127]
    return mx_ref.matmul(mx_ref.quantize(e.reshape(128, 512).astype(BF)), (c.reshape(128, 8), np.full((16, 2), 127, np.uint8))).T.reshape(-1).astype(np.float64)
CODE_VALUE, SCALE_VALUE = values_of_codes(), 2.0 ** (np.arange(256) - 127.0)
def decode(q):
    return (CODE_VALUE[q[0]].reshape(16, 8, -1, 4) * SCALE_VALUE[q[1]][:, None, :, None] + 0.0).reshape(128, -1).astype(np.float32)
def f(rng, *shape):
    return mx_ref.flush((rng.standard_normal(shape, dtype=np.float32) * np.exp2(rng.integers(-2, 3, shape[:-1] + (1,)))).astype(BF))
def wide(rng, *shape, cols=0):
    v = rng.standard_normal(shape, dtype=np.float32) * np.exp2(rng.integers(-12, 13, shape)).astype(np.float32)
    if cols: v *= np.repeat(np.exp2(rng.integers(-cols, cols + 1, shape[:-2] + (1, shape[-1] // 4))) * (rng.random(shape[:-2] + (1, shape[-1] // 4)) > 0.0625), 4, axis=-1).astype(np.float32)
    return mx_ref.flush(v.astype(BF))
C, A, R = 320, 128, 3
STEP = [1, 2, 3]
def layout(bad, sz, pr):
    g, n = np.arange(8)[:, None], np.arange(C)
    p = np.bitwise_xor.accumulate(np.concatenate([np.zeros((8, 1), np.int64), bad], axis=1), axis=1)
    odd = np.concatenate([p[g, n + sz] != p[g, n], np.zeros((8, 1), bool)], axis=1)
    up = np.where(pr < 0, C, pr)
    end = np.where(pr < 0, 0, pr + sz[g, pr])
    sib = np.where(n > pr + 1, pr + 1, np.where(n + sz < end, n + sz, C))
    pair = odd[:, :C] & odd[g, sib]
    top = np.where(odd[:, :C] & odd[g, up] & ~pair, up, n)
    for i in range(9): top = top[g, top]
    other = np.where(pair, sib, n)[g, top]
    name, rise = np.minimum(top, other), top < other
    begin = np.zeros((8, C), np.int64)
    np.maximum.at(begin, (g, name), np.where(rise, n, name))
    key = np.where(odd[:, :C], begin[g, name] * 2 * C + np.where(rise, C - 1 - n, C + n), 2 * C * C + n)
    o = np.argsort(key, axis=1, kind="stable")
    same = name[g, o[:, :-1]] == name[g, o[:, 1:]]
    return o, np.concatenate([np.where(same, o[:, 1:], -1), np.full((8, 1), -1)], axis=1)
def differences(t, o, follow):
    return (gcols(t, o).astype(np.float32) - gcols(t, follow).astype(np.float32)).astype(BF)
def big(v):
    v = v.astype(np.float32)
    v[np.abs(v) < np.float32(2.0 ** -16)] = 0
    return v.astype(BF)
def numbers_of(rng):
    return {"x": big(f(rng, N, 128, 4 * C)), "u": np.array(f(rng, N, 128, 512)), "v": np.array(f(rng, N, 128, 512))}
def weights(rng, still=[]):
    w = big(f(rng, N, 128, 2048)).reshape(N, 8, 16, 4, 8, 16, 4)
    for i in still:
        w[:, :, i] = 0
        w[:, :, :, :, :, i] = 0
    c, p = packed(np.ascontiguousarray(w).reshape(N, 128, 2048), rng)
    return {"wc": c, "ws": p}
def grown(rng):
    a, kids, way = [-1] * C, [0] * C, [0]
    back = (rng.geometric(rng.choice([0.4, 0.6, 0.8, 0.95]), C) - 1).tolist()
    for n in range(1, C):
        del way[max(1, len(way) - back[n]):]
        p = way[-1]
        a[n] = p
        kids[p] += 1
        if kids[p] == 2: way.pop()
        way.append(n)
    return np.array(a)
def chain():
    return np.arange(C) - 1
def fork(h):
    a = np.arange(C) - 1
    a[h] = 0
    return a
def comb():
    a = (np.arange(C) - 1) // 2 * 2
    a[0] = -1
    return a
def rake():
    n, h = np.arange(C), C // 2 + 1
    return np.where(n < h, n - 1, 2 * h - 2 - n)
def halves():
    a, todo = np.zeros(C, np.int64), [(0, C, -1)]
    while todo:
        lo, hi, p = todo.pop()
        a[lo] = p
        m = lo + 1 + (hi - lo) // 2
        if m > lo + 1: todo.append((lo + 1, m, lo))
        if hi > m: todo.append((m, hi, lo))
    return a
def trees(rng):
    return np.stack([np.stack([grown(rng) for g in range(8)]) for r in range(N)])
def stored(a):
    k, i = a.reshape(8 * N, C), np.arange(8 * N)
    s = np.ones((8 * N, C), np.int64)
    for n in range(C - 1, 0, -1): s[i, k[:, n]] += s[:, n]
    return {"sz": np.stack([gtable(e) for e in s.reshape(N, 8, C)]), "pr": np.stack([gtable(e) for e in a])}
def planted(rng, a, bad, still=[0]):
    d = numbers_of(rng)
    x = d["x"].reshape(N, 8, 16, C, 4)
    x[:, :, 0] = 0
    x[:, :, 0, :, 0] = np.where(bad, 1.0, -1.0).astype(np.float32).astype(BF)
    u = d["u"].reshape(N, 128, 128, 4)
    u[:, :, ::16] = 0
    for h in range(0, 128, 16): u[:, h, h, 0] = 1
    return {"x": x.reshape(N, 128, 4 * C), "u": u.reshape(N, 128, 512), "v": d["v"], **weights(rng, still), **stored(a)}
def setup_inputs(rng):
    return {**numbers_of(rng), **weights(rng), **stored(trees(rng))}
def setup_inputs_zeros(rng):
    d = numbers_of(rng)
    x = d["x"].reshape(N, 8, 16, C, 4)
    u = d["u"].reshape(N, 128, 128, 4)
    u[:, :, ::16] = 0
    e = rng.permutation(N)
    for i in range(N):
        r, body, by = e[i], np.zeros((8, 4)), np.zeros((8, 4))
        if i % 2:
            body[:] = 2.0 ** 26
            by[:] = 2.0 ** 30
        else:
            body[:2, 0] = [9 * 2.0 ** -33, 10 * 2.0 ** -33]
            by[:2, 0] = [9 * 2.0 ** -33, -8 * 2.0 ** -33]
        m = np.stack([rng.permutation(C) % 3 - 1.0 for g in range(8)])
        if i == 0: m[:] = 1
        z = m[:, None, :, None] * body[None, :, None, :]
        x[r][:, :8] = z.astype(np.float32).astype(BF)
        k = by.astype(np.float32).astype(BF)
        for h in range(0, 128, 16): u[r, h:h + 8, h] = k
    x[e[1]] = 0
    return {"x": x.reshape(N, 128, 4 * C), "u": u.reshape(N, 128, 512), "v": d["v"], **weights(rng, range(8)), **stored(trees(rng))}
def setup_inputs_chains(rng):
    a = np.broadcast_to(chain(), (N, 8, C)).copy()
    bad = np.zeros((N, 8, C), bool)
    h, e = int(rng.integers(8)), int(rng.integers(N))
    for r in range(N):
        k = np.insert(rng.permutation(np.delete(np.arange(8), h)), 5, h)
        for i, n in enumerate([1, A - 1, A, A + 1, C - 1, C]): bad[r, k[i], n - 1] = True
        bad[r, k[6]] = True
    d = planted(rng, a, bad, [0, 8])
    d["x"].reshape(N, 8, 16, C, 4)[e, h, 8, :, 0] = np.where(np.arange(C) % 2 == 1, -2.0 ** 28, 2.0 ** 28).astype(np.float32).astype(BF)
    d["v"][:, 16 * h + 8] = 0
    return d
def setup_inputs_forks(rng):
    a, bad = np.zeros((N, 8, C), np.int64), np.zeros((N, 8, C), bool)
    for r in range(N):
        k = rng.permutation(8)
        for i, h in enumerate([2, A, A + 1, C - 1]):
            a[r, k[i]] = fork(h)
            bad[r, k[i], [h - 1, C - 1]] = True
        bad[r, k[1], 0] = True
        for i, b in enumerate([comb(), rake(), halves()]):
            a[r, k[4 + i]] = b
            bad[r, k[4 + i]] = ~np.isin(np.arange(C), b)
        a[r, k[7]] = grown(rng)
        bad[r, k[7]] = True
    return planted(rng, a, bad)
def setup_inputs_spread(rng):
    d = setup_inputs(rng)
    d["x"] = big(wide(rng, N, 128, 4 * C, cols=6))
    return d
def check_inputs(d):
    b = []
    for k in ("x", "u", "v"):
        a = np.abs(d[k].astype(np.float32))
        if not (np.isfinite(a).all() and ((a == 0) | (a >= 2.0 ** -30) & (a <= 2.0 ** 30)).all()): b.append("a value of " + k)
    none, least, most = [emit(mx_ref.quantize(np.full((128, 16), k, np.float32).astype(BF)))[1][0, 0] for k in (0.0, 2.0 ** -30, 2.0 ** 30)]
    g, n = np.arange(8)[:, None], np.arange(C)
    for r in range(N):
        if ((d["wc"][r] == 0x7F) | (d["wc"][r] == 0xFF)).any(): b.append("wc: a code that is no number")
        s = mx_ref.live(d["ws"][r])
        if ((s != none) & ((s < least) | (s > most))).any(): b.append("ws: a scale out of range")
        s, p = gentries(d["sz"][r]).astype(np.int64), gentries(d["pr"][r]).astype(np.int64)
        e = n + s
        if (s < 1).any() or (e > C).any() or (s[:, 0] != C).any(): b.append("sz: a size out of range")
        above = np.max(np.where((n[:, None] < n) & (e[:, :, None] > n), n[:, None], -1), axis=1)
        if (above != p).any(): b.append("pr: not the parent")
        elif (e > e[g, np.maximum(p, 0)]).any(): b.append("sz: a subtree that goes beyond the parent's")
        elif np.max(np.sum(p[:, :, None] == n, axis=1)) > 2: b.append("pr: more than two children")
    return b
def reference(x, u, v, wc, ws, sz, pr):
    qu = [mx_ref.quantize(u[r]) for r in range(N)]
    lay = [pk(wc[r], ws[r]) for r in range(N)]
    now = [x[r] for r in range(N)]
    for t in range(R):
        sent, paths = [], []
        for r in range(N):
            q = mx_ref.quantize(now[r])
            p = mx_ref.matmul(qu[r], q)
            sent.append(q)
            paths.append(layout(p[::16] > 0, gentries(sz[r]), gentries(pr[r])))
        came = decode(join(*sent)).astype(BF)
        made = []
        for r in range(N):
            e = (r - STEP[t]) % N
            z = np.concatenate([differences(cut(came, e, 4 * C), *paths[e])[:, :4 * A], differences(now[r], *paths[r])[:, 4 * A:]], axis=1)
            q = mx_ref.quantize(np.ascontiguousarray(z))
            made.append(tile([mx_ref.matmul(pick(lay[r], np.arange(128 * b, 128 * b + 128)), q) * np.float32(0.0078125) + z[:, b::4].astype(np.float32) for b in range(4)]))
        now = made
    y, ot = np.zeros((N, 128, C), np.float32), np.zeros((N, 8, C), np.float32)
    oc, osc = np.zeros((N, 128, 4 * C), np.uint8), np.zeros((N, 16, C), np.uint8)
    for r in range(N):
        q = mx_ref.quantize(now[r])
        y[r] = mx_ref.matmul(mx_ref.quantize(v[r]), q)
        ot[r] = paths[r][0]
        oc[r], osc[r] = emit(q)
    return {"y": y, "ot": ot, "oc": oc, "osc": osc}

@@ -1,0 +1,449 @@
+from concourse.mybir import dt, AluOpType, ActivationFunctionType
+
+C, A, R = 320, 128, 3
+STEP = [1, 2, 3]
+M = 2048
+CC = 2 * 640 * M
+K = float(2 ** 22)
+BIG = float(2 ** 24)
+SC = 2.0 ** -23
+F32, BF, I32, U16, Q4, U8 = "float32", "bfloat16", "int32", "uint16", "float8_e4m3fn_x4", "uint8"
+LISTS = ["lpm", "lend", "lpar", "lp1", "lrs", "ldr", "lq", "lpp", "lpost", "lsig", "lb", "lpos", "lvn"]
+
+SCRATCH = {"ps": ("psum", [128, 4096], F32)}
+for _d, _l in (
+    (BF, "xb:3840 db:3840 x128:1280 z:1280 z128:1280 g2o:784 g2a:528 ub:512 vb:512 ones:516 e0:516 e1:516 junk:3360 "
+         "cvp m2 q p:336 ph:336 pp osg hh:336 pcv kk yy jp ycv jcv sg:336"),
+    (Q4, "qz qu:128 qu2:128 qv:128 qw:512 qe:512 qx0 qx1 qx2 qx3 lc0 lc1 lc2"),
+    (U8, "zs su:128 su2:128 sv:128 sw:512 se:512 sx0 sx1 sx2 sx3 ls0 ls1 ls2"),
+    (I32, "szw:20 prw:20 ip:4 pi:8 mi:32 mj:32 ri:20 si:20 rl:20 sl:20"),
+    (U16, "li:%d llv:40 lu:8 ll0:34 ll1:34 ll2:34 lo0:96 lo1:96 lo2:96" % (20 * len(LISTS))),
+    (F32, "pf:8 col:16 i16:20 ii:16 nw:20 nb:20 n1k:20 ba:32 bb:32 blk:32 cv16 cv4 tab:648 cs:1856 c2 tt:968 endw:20 "
+          "s1:20 s2:20 s3:20 s4:20 s6:20 acc:20 endr wr r0 cv cvb ssw sswp pre dd:328 a2 kw:20 vn vs cc:328 ua vbk "
+          "ff gg fn gn d1 npb:20 lv:40 lenr vf tg orow ot1 ot2 ys"),
+):
+    for _e in _l.split():
+        SCRATCH[_e.split(":")[0]] = ("sbuf", [128, int(_e.split(":")[1]) if ":" in _e else C], _d)
+
+NDMA = 30
+SEMAPHORES = (["cv", "cs", "ct", "cg", "left"] + ["qa%d" % t for t in range(R)] + ["la%d" % t for t in range(R)]
+              + ["d%d" % i for i in range(NDMA)])
+OP = AluOpType
+AF = ActivationFunctionType
+
+
+def rank_program(g, core, T, topo):
+    rank = T.rank_of(core)
+    if rank is None:
+        return
+    N = len(T.cores)
+    eng = {"v": g.vector, "s": g.scalar, "t": g.tensor, "g": g, "y": g.sync}
+    semof = {"v": "cv", "s": "cs", "t": "ct", "g": "cg"}
+    count = {}
+    known = {k: {} for k in eng}
+    hist = {}
+    ndma = [0]
+
+    def a(name, lo=0, hi=None, step=1, rev=False):
+        if name in LISTS:
+            name, lo, hi = "li", 20 * LISTS.index(name), 20 * LISTS.index(name) + 20
+        if hi is None:
+            hi = SCRATCH[name][1][1]
+        bits = 0
+        if name == "ps":
+            bits = 1 << (lo // 512)
+        elif step == 1:
+            bits = ((1 << (hi - lo)) - 1) << lo
+        else:
+            for c in range(lo, hi, step):
+                bits |= 1 << c
+        if rev:
+            last = lo + (hi - lo - 1) // step * step
+            v = T[name][:, last::-step] if lo - step < 0 else T[name][:, last:lo - step:-step]
+        elif step == 1:
+            v = T[name][:, lo:hi]
+        else:
+            v = T[name][:, lo:hi:step]
+        return (v, [(name, bits)])
+
+    def ind(win, off):
+        return (win[0].indirect(off[0]), win[1] + off[1], len(win[1]))
+
+    def wait(qn, tok):
+        if known[qn].get(tok[0], 0) >= tok[1]:
+            return
+        eng[qn].wait_ge(T.sem[tok[0]], tok[1])
+        for k2, v2 in tok[2].items():
+            if known[qn].get(k2, 0) < v2:
+                known[qn][k2] = v2
+        known[qn][tok[0]] = tok[1]
+
+    def run(qn, fn, outs, ins, dma=False, inc=True):
+        wr, rd = [], []
+        for o in outs:
+            n = o[2] if len(o) > 2 else len(o[1])
+            wr += o[1][:n]
+            rd += o[1][n:]
+        for i in ins:
+            for e in i[1]:
+                (wr if e[0] == "ps" else rd).append(e)
+        need = {}
+        for lst, both in ((wr, True), (rd, False)):
+            for name, bits in lst:
+                for kind, b, tok in hist.get(name, []):
+                    if b & bits and (both or kind == "w"):
+                        if tok[0] not in need or need[tok[0]][1] < tok[1]:
+                            need[tok[0]] = tok
+        for tok in sorted(need.values(), key=lambda t: -len(t[2])):
+            wait(qn, tok)
+        call = fn()
+        if not inc:
+            return
+        if dma:
+            s, n = "d%d" % ndma[0], 16
+            ndma[0] += 1
+        else:
+            s, n = semof[qn], 1
+        call.then_inc(T.sem[s], n)
+        count[s] = count.get(s, 0) + n
+        tok = (s, count[s], dict(known[qn]))
+        for name, bits in wr:
+            h = [[k2, b & ~bits, t2] for k2, b, t2 in hist.get(name, []) if b & ~bits]
+            hist[name] = h + [["w", bits, tok]]
+        for name, bits in rd:
+            hist.setdefault(name, []).append(["r", bits, tok])
+
+    def aps(*xs):
+        return [x for x in xs if isinstance(x, tuple)]
+
+    def val(x):
+        return x[0] if isinstance(x, tuple) else x
+
+    def ts(o, i, s1, op0, s2=None, op1=None):
+        if op1 is None:
+            run("v", lambda: g.vector.tensor_scalar(o[0], i[0], val(s1), None, op0), [o], aps(i, s1))
+        else:
+            run("v", lambda: g.vector.tensor_scalar(o[0], i[0], val(s1), val(s2), op0, op1), [o], aps(i, s1, s2))
+
+    def tt(o, i0, i1, op):
+        run("v", lambda: g.vector.tensor_tensor(o[0], i0[0], i1[0], op), [o], [i0, i1])
+
+    def cp(o, i):
+        run("v", lambda: g.vector.tensor_copy(o[0], i[0]), [o], [i])
+
+    def ms(o, c):
+        run("v", lambda: g.vector.memset(o[0], c), [o], [])
+
+    def scan(o, d0, d1, init, op0, op1):
+        run("v", lambda: g.vector.tensor_tensor_scan(o[0], d0[0], d1[0], val(init), op0, op1), [o], aps(d0, d1, init))
+
+    def act(o, i, f=None, bias=None, scale=None, acc=None):
+        kw = {}
+        if bias is not None:
+            kw["bias"] = val(bias)
+        if scale is not None:
+            kw["scale"] = scale
+        if acc is not None:
+            kw["accum_out"] = acc[0]
+        if f is None:
+            f = AF.Copy if bias is None else AF.Identity
+        run("s", lambda: g.scalar.activation(o[0], i[0], f, **kw), aps(o, acc), aps(i, bias))
+
+    def quant(qn, sn, lo, hi, src):
+        o, s = a(qn, lo, hi), a(sn, lo, hi)
+        run("v", lambda: g.vector.quantize_mx(o[0], s[0], src[0]), [o, s], [src])
+
+    def mm(bank, lq, ls, llo, rq, rs, lo, hi):
+        o = a("ps", 512 * bank, 512 * bank + hi - lo)
+        x = [a(lq, llo, llo + 128), a(ls, llo, llo + 128), a(rq, lo, hi), a(rs, lo, hi)]
+        run("t", lambda: g.tensor.matmul_mx(o[0], x[0][0], x[1][0], x[2][0], x[3][0], True, True), [o], x)
+
+    def iota(o, pat, base, cm, small=True):
+        if small:
+            run("g", lambda: g.iota(o[0], pat, base, cm, allow_small_or_imprecise_dtypes=True), [o], [])
+        else:
+            run("g", lambda: g.iota(o[0], pat, base, cm), [o], [])
+
+    def dma(qn, out, in_, outs, ins):
+        run(qn, lambda: eng[qn].dma_start(out, in_), outs, ins, dma=True)
+
+    def u8(x):
+        return x[0].bitcast(dt.uint8)
+
+    def send(t, src, dst, sem):
+        to = T.cores[(rank + STEP[t]) % N]
+        rid, pid, _ = topo.addr(to)
+        m = topo.mask(core, to)
+        run("g", lambda: g.remote_dma(dst, src[0], T.sem[sem], T.sem.left, pid, rid, m), [], [src], inc=False)
+        count["left"] = count.get("left", 0) + len(topo.engines(core, to))
+
+    def conv(o, row, table="cv16", lo=0, hi=C):
+        scan(a(o, lo, hi), a(table, lo, hi), row, 0.0, OP.add, OP.max)
+
+    def w16(name):
+        return a(name, 15, C, 16)
+
+    def col(i):
+        return a("col", i, i + 1)
+
+    def bank(b, n):
+        return a("ps", 512 * b, 512 * b + n)
+
+    for t in range(R):
+        frm = T.cores[(rank - STEP[t]) % N]
+        ne = len(topo.engines(frm, core))
+        count["qa%d" % t] = 2 * ne
+        count["la%d" % t] = ne
+        for nm in ("lc%d" % t, "ls%d" % t):
+            hist[nm] = [["w", a(nm)[1][0][1], ("qa%d" % t, 2 * ne, {})]]
+        hist["ll%d" % t] = [["w", a("ll%d" % t)[1][0][1], ("la%d" % t, ne, {})]]
+
+    dma("y", T.szw[:], T.sz[:], [a("szw")], [])
+    dma("s", T.prw[:], T.pr[:], [a("prw")], [])
+    dma("y", T.ub[:], T.u[:], [a("ub")], [])
+    dma("s", T.xb[:, 0:4 * C], T.x[:], [a("xb", 0, 4 * C)], [])
+    dma("y", T.xb[:, 4 * C:8 * C], T.x[:], [a("xb", 4 * C, 8 * C)], [a("xb", 0, 4)])
+    dma("y", u8(a("qw")), T.wc[:], [a("qw")], [])
+    dma("y", T.sw[:], T.ws[:], [a("sw")], [])
+    dma("y", T.vb[:], T.v[:], [a("vb")], [])
+
+    iota(a("ip", 0, 1), [[0, 1]], 0, 1, small=False)
+    iota(a("i16"), [[16, 20]], 0, 0)
+    iota(a("ii"), [[1, 16]], 16, 0)
+    iota(a("tab"), [[1, 648]], 0, 0)
+    ms(a("m2"), -2.0)
+    ms(a("p", 0, 1), 2.0)
+    ms(a("ph", 0, 1), 0.5)
+    ms(a("dd", 0, 1), 0.0)
+    ms(a("sg", C, C + 1), -1.0)
+    ms(a("hh", C, C + 1), 1.0)
+    ms(a("cc", C, C + 1), 1.0)
+    ms(a("g2o", 768, 784), 0.0)
+    ts(a("pi", 0, 1), a("ip", 0, 1), 15, OP.bitwise_and)
+    ts(a("pi", 1, 2), a("ip", 0, 1), 2, OP.arith_shift_right, 3, OP.bitwise_and)
+    ts(a("pi", 2, 3), a("ip", 0, 1), 3, OP.bitwise_and)
+    cp(a("lu"), a("i16", 0, 8))
+    cp(a("pf", 0, 3), a("pi", 0, 3))
+    ts(a("nw"), a("i16"), a("pf", 0, 1), OP.add)
+    ts(a("mi", 0, 16), a("ii"), a("pf", 0, 1), OP.subtract)
+    ts(a("mi", 16, 32), a("ii"), a("pf", 1, 2), OP.subtract)
+    ts(a("lpm"), a("i16"), 0.0, OP.mult, a("pf", 0, 1), OP.add)
+    ts(a("pf", 4, 5), a("pf", 0, 1), 15.0, OP.is_lt, K, OP.mult)
+    ts(a("pf", 5, 6), a("pf", 1, 2), 3.0, OP.is_lt, -4 * K, OP.mult)
+    ts(a("mj", 0, 16), a("mi", 0, 16), 15, OP.bitwise_and)
+    ts(a("mj", 16, 32), a("mi", 16, 32), 3, OP.bitwise_and)
+    ts(a("nb"), a("nw"), -1.0, OP.mult, -0.5, OP.add)
+    ts(a("ba"), a("mj"), 0.0, OP.is_equal, -BIG, OP.mult)
+    ts(a("bb"), a("mj"), 1.0, OP.is_equal, K, OP.mult)
+    kf = a("pf", 4, 5)
+    ts(col(0), kf, -1.0, OP.mult)
+    ts(col(1), kf, (C - 1) / 2.0, OP.add)
+    tt(a("blk"), a("ba"), a("bb"), OP.add)
+    ts(col(2), kf, -4.0 / K, OP.mult)
+    ts(col(3), kf, -1.0 / M, OP.mult, float(CC // M), OP.add)
+    ts(col(5), kf, 4.0 / K, OP.mult, 1.0, OP.add)
+    ts(col(6), kf, -4096.0 / K, OP.mult, 512.0, OP.add)
+    ts(a("n1k"), a("nw"), 1.0 / 1024, OP.mult)
+    tt(col(4), a("pf", 5, 6), a("pf", 2, 3), OP.add)
+    act(a("cv16"), ind(a("blk", 0, 16), a("lpm")))
+
+    tt(a("endw"), a("nw"), a("szw"), OP.add)
+    cp(a("lpar"), a("prw"))
+    tt(a("s1"), a("nw"), a("prw"), OP.subtract)
+    cp(a("lend"), a("endw"))
+    ts(a("s2"), a("s1"), 1.0, OP.is_gt)
+    tt(a("s4"), a("s1"), a("endw"), OP.add)
+    cp(a("endr"), ind(a("tab"), a("lend")))
+    off = 0
+    for c in range(19, -1, -1):
+        n = 16 * c + 16
+        act(a("junk", off, off + n), a("endr", 0, n), AF.Sign, bias=a("nb", c, c + 1), acc=a("acc", c, c + 1))
+        off += n
+    act(a("cvp"), a("cv16"), scale=4.0 / K)
+    quant("qu", "su", 0, 128, a("ub"))
+    ts(a("ldr"), a("s4"), -1.0, OP.add)
+    ts(a("lp1"), a("prw"), 1.0, OP.add)
+    tt(a("s3"), a("s2"), a("szw"), OP.mult)
+    lu = a("lu")
+    run("v", lambda: g.vector.tensor_copy(T.qu2[:, 0:128].bitcast(dt.uint32),
+                                          T.qu[:, 0:128].bitcast(dt.uint32).indirect(lu[0])),
+        [a("qu2")], [a("qu"), lu])
+    run("v", lambda: g.vector.tensor_copy(T.su2[:, 0:128], T.su[:, 0:128].indirect(lu[0])), [a("su2")], [a("su"), lu])
+    tt(a("s4"), a("endw"), a("s3"), OP.subtract)
+    quant("qx0", "sx0", 0, C, a("xb", 0, 4 * C))
+    cp(a("lrs"), a("s4"))
+
+    def spread(t):
+        send(t, (u8(a("qx%d" % t)), a("qx%d" % t)[1]), u8(a("lc%d" % t)), "qa%d" % t)
+        send(t, a("sx%d" % t), a("ls%d" % t)[0], "qa%d" % t)
+
+    def defects(lo, hi, b):
+        ts(a("q", lo, hi), bank(b, hi - lo), 0.0, OP.is_gt, 0.5, OP.subtract)
+
+    mm(0, "qu2", "su2", 0, "qx0", "sx0", 0, C)
+    spread(0)
+    cp(a("r0"), ind(a("tab"), a("ldr")))
+    defects(0, C, 0)
+    tt(a("wr"), ind(a("endr"), a("lpar")), a("r0"), OP.subtract)
+    iota(a("c2"), [[0, C]], M * 2 - 1, 0)
+    iota(a("tt"), [[0, 968]], CC // 2 - 1, 0)
+    iota(a("ones"), [[0, 516]], 1, 0)
+    for k in range(2):
+        o = a("e%d" % k)
+        run("g", lambda: g.affine_select(o[0], T.ones[:], [[1, 516]], OP.is_equal, 0.0, -2 - k, -4), [o], [a("ones")])
+    iota(a("xb", 8 * C, 12 * C), [[0, 4 * C]], 0, 0)
+    iota(a("db", 8 * C, 12 * C), [[0, 4 * C]], 0, 0)
+
+    def post_lists():
+        tt(a("s6"), a("i16"), a("acc"), OP.subtract)
+        ts(a("s6"), a("s6"), 0.5, OP.mult, 8.0, OP.add)
+        tt(a("s2"), a("s6"), a("szw"), OP.add)
+        cp(a("lq"), a("s6"))
+        ts(a("lpp"), a("s2"), -1.0, OP.add)
+        cp(ind(a("r0"), a("lpp")), a("tab", 0, C))
+        conv("cv", a("r0"))
+        ts(a("lpost"), w16("cv"), col(0), OP.add)
+
+    for t in range(R):
+        lo, ll = "lo%d" % t, "ll%d" % t
+        last = t == R - 1
+        P = a("ph", 0, C)
+        scan(a("ph", 1, C + 1), a("q"), a("m2"), 0.5, OP.mult, OP.mult)
+        scan(a("p", 1, C + 1), a("q"), a("m2"), 2.0, OP.mult, OP.mult)
+        pw = a("ph", 0, C + 1)
+        if t:
+            act(a("pp"), ind(pw, a("lpost")))
+        else:
+            for e, n, f in ((0, 512, -0.5), (512, 512, -0.5), (1024, 512, 0.5), (1536, C, 1.0)):
+                act(a("cs", e, e + n), a("tab", 0, n), bias=f * (2 - CC) * SC, scale=f * 2 * M * SC)
+        tt(a("osg"), ind(pw, a("lend")), a("p", 0, C), OP.mult)
+        tt(a("hh", 0, C), ind(pw, a("lp1")), a("osg"), OP.mult)
+        tt(a("ssw"), ind(a("hh", 0, C + 1), a("lrs")), a("wr"), OP.mult)
+        if t == 0:
+            post_lists()
+            act(a("pp"), ind(pw, a("lpost")))
+        act(a("sswp"), ind(a("ssw"), a("lpost")))
+        tt(a("kk"), a("q"), P, OP.min)
+        scan(a("pre"), a("ssw"), P, 0.0, OP.add, OP.subtract)
+        tt(a("yy"), a("kk"), a("osg"), OP.add)
+        scan(a("dd", 1, C + 1), a("sswp"), a("pp"), 0.0, OP.add, OP.subtract)
+        act(a("jp"), ind(a("yy"), a("lpar")), bias=-1.0)
+        conv("ycv", a("yy"), "cvp")
+        conv("pcv", P, "cvp")
+        tt(a("a2"), ind(a("dd", 0, C + 1), a("lq")), a("pre"), OP.subtract)
+        conv("jcv", a("jp"), "cvp")
+        ts(a("s2"), w16("ycv"), 1.0, OP.add, col(5), OP.min)
+        ts(a("kw"), w16("pcv"), col(2), OP.add)
+        tt(a("s2"), a("s2"), w16("jcv"), OP.max)
+        tt(a("kw"), a("kw"), a("szw"), OP.mult)
+        tt(a("s2"), a("s2"), a("n1k"), OP.add)
+        ts(a("lvn"), a("s2"), 1024.0, OP.mult, col(6), OP.add)
+        act(a("vn"), ind(a("cs"), a("lvn")))
+        act(a("d1"), a("osg"), bias=float(M + 2), scale=2.0)
+        if t == 0:
+            act(a("cv4"), ind(a("blk", 16, 32), a("lpm")))
+        conv("cv", a("a2"))
+        tt(a("s1"), a("kw"), w16("cv"), OP.subtract)
+        ts(a("lsig"), a("s1"), col(1), OP.add)
+        cp(ind(a("vs"), a("lsig")), a("vn"))
+        act(a("ua"), a("vs"), AF.Abs)
+        act(a("sg", 0, C), a("vs"), AF.Sign)
+        ts(a("cc", 0, C), a("vs"), 0.0, OP.is_lt, 2 * SC, OP.max)
+        scan(a("ff"), a("cc", 0, C), a("vs"), 1.0, OP.add, OP.min)
+        act(a("fn"), ind(a("ff"), a("lsig")), scale=1 / SC)
+        tt(a("vbk"), a("ua"), a("sg", 1, C + 1), OP.mult)
+        scan(a("gg", rev=True), a("cc", 1, C + 1, rev=True), a("vbk", rev=True), 1.0, OP.add, OP.min)
+        act(a("gn"), ind(a("gg"), a("lsig")), scale=1 / SC)
+        scan(a("tt", 0, 2 * C, 2, rev=True), a("c2"), a("osg", rev=True), float(2 * C - 2 * M * C - 2 + CC),
+             OP.add, OP.subtract)
+        conv("cv", a("fn"))
+        conv("cvb", a("gn"))
+        tt(a("ri"), w16("cv"), w16("cvb"), OP.min)
+        tt(a("si"), w16("cv"), w16("cvb"), OP.add)
+        ts(a("rl"), a("ri"), M - 1, OP.bitwise_and)
+        ts(a("sl"), a("si"), M - 1, OP.bitwise_and, 1, OP.arith_shift_right)
+        ts(a("npb"), a("rl"), 2.5, OP.is_lt, float(C), OP.mult)
+        ts(a("lb"), a("ri"), 1.0 / M, OP.mult, col(3), OP.add)
+        tt(a("lv", 0, 20), a("npb"), a("sl"), OP.min)
+        tt(a("lv", 20, 40), a("npb"), a("nw"), OP.add)
+        cp(a("llv"), a("lv"))
+        ts(a("lenr"), ind(a("tab"), a("llv", 0, 20)), 2.0, OP.mult)
+        act(a("vf"), ind(a("tab"), a("llv", 20, 40)))
+        if t == 0:
+            for b in range(4):
+                s = 2 - 2 * (b // 2)
+                quant("qe", "se", 128 * b, 128 * b + 128, a("e%d" % (b % 2), s, s + 512))
+        for b in range(4):
+            mm(4 + b, "qe", "se", 128 * b, "lc%d" % t, "ls%d" % t, 0, C)
+        for b in range(4):
+            act(a("db", b, 4 * C, 4), bank(4 + b, C))
+        dma("y", T.db[:, 4 * C:8 * C], T.db[:, 0:4 * C], [a("db", 4 * C, 8 * C)], [a("db", 0, 4 * C)])
+        scan(a("tt", 2 * C + 1, 3 * C + 1), a("lenr"), a("d1"), float(CC // 2 - 1), OP.add, OP.subtract)
+        cp(a("tg"), ind(a("tt"), a("lb")))
+        conv("cv", a("tg"))
+        tt(a("s1"), w16("cv"), a("ri"), OP.add)
+        ts(a("lpos"), a("s1"), 0.5, OP.mult, col(0), OP.add)
+        cp(ind(a("orow"), a("lpos")), a("vf"))
+        conv("cv", a("orow", 0, 136), "cv4", 0, 136)
+        conv("cvb", a("orow", A, C), "cv4", A, C)
+        ts(a(lo, 0, 34), a("cv", 3, 136, 4), 4.0, OP.mult, col(4), OP.add)
+        send(t, a(lo, 0, 34), a(ll)[0], "la%d" % t)
+        ts(a(lo, 48, 96), a("cvb", A + 3, C, 4), 4.0, OP.mult, col(4), OP.add)
+        wa, wb = a("xb", 0, 8 * C), a("xb", 4 * C, 12 * C)
+        for c0, c1 in ((0, 10), (10, 30), (30, 48)):
+            act(a("g2o", 16 * c0, 16 * c1), ind(wb, a(lo, 48 + c0, 48 + c1)))
+        for c0, c1 in ((0, 8), (8, 28), (28, 48)):
+            e0, e1 = 4 * A + 16 * c0, 4 * A + 16 * c1
+            tt(a("z", e0, e1), ind(wa, a(lo, 48 + c0, 48 + c1)), a("g2o", 16 * c0 + 4, 16 * c1 + 4), OP.subtract)
+            act(a("z128", e0, e1), a("z", e0, e1), scale=128.0)
+        quant("qz", "zs", A, C, a("z", 4 * A, 4 * C))
+        for b in range(4):
+            mm(b, "qw", "sw", 128 * b, "qz", "zs", A, C)
+        if last:
+            ts(a("ot1"), a("orow"), float(C), OP.is_ge, -float(C), OP.mult)
+        if t == 0:
+            quant("qv", "sv", 0, 128, a("vb"))
+        da, dbb = a("db", 0, 8 * C), a("db", 4 * C, 12 * C)
+        for c0, c1 in ((0, 10), (10, 33)):
+            act(a("g2a", 16 * c0, 16 * c1), ind(dbb, a(ll, c0, c1)))
+        for b in range(4):
+            tt(a("x128", 4 * A + b, 4 * C, 4), bank(b, C - A), a("z128", 4 * A + b, 4 * C, 4), OP.add)
+        qn, sn = "qx%d" % (t + 1), "sx%d" % (t + 1)
+        lq, ls = ("qv", "sv") if last else ("qu2", "su2")
+        ts(a("xb", 4 * A, 4 * C), a("x128", 4 * A, 4 * C), 0.0078125, OP.mult)
+        quant(qn, sn, A, C, a("xb", 4 * A, 4 * C))
+        mm(0, lq, ls, 0, qn, sn, A, C)
+        if last:
+            dma("y", T.oc[:, 4 * A:4 * C], u8(a(qn, A, C)), [], [a(qn, A, C)])
+        for c0, c1 in ((0, 8), (8, 32)):
+            e0, e1 = 16 * c0, 16 * c1
+            tt(a("z", e0, e1), ind(da, a(ll, c0, c1)), a("g2a", e0 + 4, e1 + 4), OP.subtract)
+            act(a("z128", e0, e1), a("z", e0, e1), scale=128.0)
+        quant("qz", "zs", 0, A, a("z", 0, 4 * A))
+        for b in range(4):
+            mm(4 + b, "qw", "sw", 128 * b, "qz", "zs", 0, A)
+        if last:
+            act(a("ys", A, C), bank(0, C - A))
+            dma("s", T.y[:, A:C], T.ys[:, A:C], [], [a("ys", A, C)])
+            tt(a("ot2"), a("ot1"), a("orow"), OP.add)
+            dma("y", T.ot[:], T.ot2[0:128:16, :], [], [a("ot2")])
+        else:
+            defects(A, C, 0)
+        for b in range(4):
+            tt(a("x128", b, 4 * A, 4), bank(4 + b, A), a("z128", b, 4 * A, 4), OP.add)
+        ts(a("xb", 0, 4 * A), a("x128", 0, 4 * A), 0.0078125, OP.mult)
+        quant(qn, sn, 0, A, a("xb", 0, 4 * A))
+        mm(1, lq, ls, 0, qn, sn, 0, A)
+        if last:
+            cp(a("ys", 0, A), bank(1, A))
+            dma("y", T.oc[:, 0:4 * A], u8(a(qn, 0, A)), [], [a(qn, 0, A)])
+            for k in range(4):
+                dma("ys"[k % 2], T.osc[4 * k:4 * k + 4, :], T[sn][32 * k:32 * k + 4, :], [], [a(sn)])
+            dma("s", T.y[:, 0:A], T.ys[:, 0:A], [], [a("ys", 0, A)])
+        else:
+            spread(t + 1)
+            dma("y", T.xb[:, 4 * C:8 * C], T.xb[:, 0:4 * C], [a("xb", 4 * C, 8 * C)], [a("xb", 0, 4 * C)])
+            defects(0, A, 1)
+
+    for s, n in count.items():
+        g.wait_ge(T.sem[s], n)

@@ -9,6 +9,7 @@ BIG = float(2 ** 24)
 SC = 2.0 ** -23
 F32, BF, I32, U16, Q4, U8 = "float32", "bfloat16", "int32", "uint16", "float8_e4m3fn_x4", "uint8"
 LISTS = ["lpm", "lend", "lpar", "lp1", "lrs", "ldr", "lq", "lpp", "lpost", "lsig", "lb", "lpos", "lvn"]
+LQ = 20 * LISTS.index("lq")
 
 SCRATCH = {"ps": ("psum", [128, 4096], F32)}
 for _d, _l in (
@@ -16,11 +17,11 @@ for _d, _l in (
          "cvp m2 q p:336 ph:336 pp osg hh:336 pcv kk yy jp ycv jcv sg:336"),
     (Q4, "qz qu:128 qu2:128 qv:128 qw:512 qe:512 qx0 qx1 qx2 qx3 lc0 lc1 lc2"),
     (U8, "zs su:128 su2:128 sv:128 sw:512 se:512 sx0 sx1 sx2 sx3 ls0 ls1 ls2"),
-    (I32, "szw:20 prw:20 ip:4 pi:8 mi:32 mj:32 ri:20 si:20 rl:20 sl:20"),
+    (I32, "szw:20 prw:20 ip:4 pi:8 mi:32 mj:32 ri:20 si:20 sl:20"),
     (U16, "li:%d llv:40 lu:8 ll0:34 ll1:34 ll2:34 lo0:96 lo1:96 lo2:96" % (20 * len(LISTS))),
     (F32, "pf:8 col:16 i16:20 ii:16 nw:20 nb:20 n1k:20 ba:32 bb:32 blk:32 cv16 cv4 tab:648 cs:1856 c2 tt:968 endw:20 "
-          "s1:20 s2:20 s3:20 s4:20 s6:20 acc:20 endr wr r0 cv cvb ssw sswp pre dd:328 a2 kw:20 vn vs cc:328 ua vbk "
-          "ff gg fn gn d1 npb:20 lv:40 lenr vf tg orow ot1 ot2 ys"),
+          "s1:20 s2:20 s3:20 s4:20 s6:40 hl:40 acc:20 base:40 ocw:20 endr wr r0 cv cvb ssw sswp pre dd:328 a2 kw:20 "
+          "vn vs cc:328 ua vbk ff gg fn gn rn d1 npb:20 lv:40 lenr vf tg orow ys"),
 ):
     for _e in _l.split():
         SCRATCH[_e.split(":")[0]] = ("sbuf", [128, int(_e.split(":")[1]) if ":" in _e else C], _d)
@@ -228,38 +229,35 @@ def rank_program(g, core, T, topo):
     ts(a("mi", 0, 16), a("ii"), a("pf", 0, 1), OP.subtract)
     ts(a("mi", 16, 32), a("ii"), a("pf", 1, 2), OP.subtract)
     ts(a("lpm"), a("i16"), 0.0, OP.mult, a("pf", 0, 1), OP.add)
+    ts(a("nb"), a("i16"), a("pf", 0, 1), OP.add, -1.0, OP.mult)
     ts(a("pf", 4, 5), a("pf", 0, 1), 15.0, OP.is_lt, K, OP.mult)
     ts(a("pf", 5, 6), a("pf", 1, 2), 3.0, OP.is_lt, -4 * K, OP.mult)
     ts(a("mj", 0, 16), a("mi", 0, 16), 15, OP.bitwise_and)
     ts(a("mj", 16, 32), a("mi", 16, 32), 3, OP.bitwise_and)
-    ts(a("nb"), a("nw"), -1.0, OP.mult, -0.5, OP.add)
+    ts(a("nb"), a("nb"), -0.5, OP.add)
+    ts(a("hl", 0, 20), a("i16"), 16.0, OP.add)
+    ts(a("base", 0, 20), a("nw"), float(M), OP.mult, 1.0 - CC // 2, OP.add)
+    kf = a("pf", 4, 5)
+    tt(a("endw"), a("nw"), a("szw"), OP.add)
     ts(a("ba"), a("mj"), 0.0, OP.is_equal, -BIG, OP.mult)
     ts(a("bb"), a("mj"), 1.0, OP.is_equal, K, OP.mult)
-    kf = a("pf", 4, 5)
     ts(col(0), kf, -1.0, OP.mult)
-    ts(col(1), kf, (C - 1) / 2.0, OP.add)
-    tt(a("blk"), a("ba"), a("bb"), OP.add)
-    ts(col(2), kf, -4.0 / K, OP.mult)
-    ts(col(3), kf, -1.0 / M, OP.mult, float(CC // M), OP.add)
-    ts(col(5), kf, 4.0 / K, OP.mult, 1.0, OP.add)
-    ts(col(6), kf, -4096.0 / K, OP.mult, 512.0, OP.add)
-    ts(a("n1k"), a("nw"), 1.0 / 1024, OP.mult)
-    tt(col(4), a("pf", 5, 6), a("pf", 2, 3), OP.add)
-    act(a("cv16"), ind(a("blk", 0, 16), a("lpm")))
-
-    tt(a("endw"), a("nw"), a("szw"), OP.add)
-    cp(a("lpar"), a("prw"))
-    tt(a("s1"), a("nw"), a("prw"), OP.subtract)
     cp(a("lend"), a("endw"))
-    ts(a("s2"), a("s1"), 1.0, OP.is_gt)
-    tt(a("s4"), a("s1"), a("endw"), OP.add)
+    tt(a("s1"), a("nw"), a("prw"), OP.subtract)
+    tt(a("blk"), a("ba"), a("bb"), OP.add)
+    cp(a("lpar"), a("prw"))
     cp(a("endr"), ind(a("tab"), a("lend")))
     off = 0
     for c in range(19, -1, -1):
         n = 16 * c + 16
         act(a("junk", off, off + n), a("endr", 0, n), AF.Sign, bias=a("nb", c, c + 1), acc=a("acc", c, c + 1))
         off += n
+    act(a("cv16"), ind(a("blk", 0, 16), a("lpm")))
     act(a("cvp"), a("cv16"), scale=4.0 / K)
+    for e, n, f in ((0, 512, -0.5), (512, 512, -0.5), (1024, 512, 0.5), (1536, C, 1.0)):
+        act(a("cs", e, e + n), a("tab", 0, n), bias=f * (2 - CC) * SC, scale=f * 2 * M * SC)
+    ts(a("s2"), a("s1"), 1.0, OP.is_gt)
+    tt(a("s4"), a("s1"), a("endw"), OP.add)
     quant("qu", "su", 0, 128, a("ub"))
     ts(a("ldr"), a("s4"), -1.0, OP.add)
     ts(a("lp1"), a("prw"), 1.0, OP.add)
@@ -280,29 +278,28 @@ def rank_program(g, core, T, topo):
     def defects(lo, hi, b):
         ts(a("q", lo, hi), bank(b, hi - lo), 0.0, OP.is_gt, 0.5, OP.subtract)
 
+    def unit(t, b):
+        if t == 0:
+            s = 2 - 2 * (b // 2)
+            quant("qe", "se", 128 * b, 128 * b + 128, a("e%d" % (b % 2), s, s + 512))
+
+    def rn(lo, hi):
+        tt(a("rn", lo, hi), a("fn", lo, hi), a("gn", lo, hi), OP.min)
+
     mm(0, "qu2", "su2", 0, "qx0", "sx0", 0, C)
     spread(0)
+    ts(a("s6", 0, 20), a("szw"), 2.0, OP.mult, -2.0, OP.add)
     cp(a("r0"), ind(a("tab"), a("ldr")))
+    tt(a("hl", 20, 40), a("hl", 0, 20), a("s6", 0, 20), OP.add)
     defects(0, C, 0)
-    tt(a("wr"), ind(a("endr"), a("lpar")), a("r0"), OP.subtract)
-    iota(a("c2"), [[0, C]], M * 2 - 1, 0)
-    iota(a("tt"), [[0, 968]], CC // 2 - 1, 0)
     iota(a("ones"), [[0, 516]], 1, 0)
     for k in range(2):
         o = a("e%d" % k)
         run("g", lambda: g.affine_select(o[0], T.ones[:], [[1, 516]], OP.is_equal, 0.0, -2 - k, -4), [o], [a("ones")])
-    iota(a("xb", 8 * C, 12 * C), [[0, 4 * C]], 0, 0)
+    iota(a("c2"), [[0, C]], M * 2 - 1, 0)
+    iota(a("tt"), [[0, 968]], CC // 2 - 1, 0)
     iota(a("db", 8 * C, 12 * C), [[0, 4 * C]], 0, 0)
-
-    def post_lists():
-        tt(a("s6"), a("i16"), a("acc"), OP.subtract)
-        ts(a("s6"), a("s6"), 0.5, OP.mult, 8.0, OP.add)
-        tt(a("s2"), a("s6"), a("szw"), OP.add)
-        cp(a("lq"), a("s6"))
-        ts(a("lpp"), a("s2"), -1.0, OP.add)
-        cp(ind(a("r0"), a("lpp")), a("tab", 0, C))
-        conv("cv", a("r0"))
-        ts(a("lpost"), w16("cv"), col(0), OP.add)
+    dma("y", T.xb[:, 8 * C:12 * C], T.db[:, 8 * C:12 * C], [a("xb", 8 * C, 12 * C)], [a("db", 8 * C, 12 * C)])
 
     for t in range(R):
         lo, ll = "lo%d" % t, "ll%d" % t
@@ -313,42 +310,73 @@ def rank_program(g, core, T, topo):
         pw = a("ph", 0, C + 1)
         if t:
             act(a("pp"), ind(pw, a("lpost")))
+            conv("pcv", P, "cvp")
         else:
-            for e, n, f in ((0, 512, -0.5), (512, 512, -0.5), (1024, 512, 0.5), (1536, C, 1.0)):
-                act(a("cs", e, e + n), a("tab", 0, n), bias=f * (2 - CC) * SC, scale=f * 2 * M * SC)
+            tt(a("wr"), ind(a("endr"), a("lpar")), a("r0"), OP.subtract)
         tt(a("osg"), ind(pw, a("lend")), a("p", 0, C), OP.mult)
+        tt(a("kk", 0, 160), a("q", 0, 160), a("ph", 0, 160), OP.min)
+        if t == 0:
+            tt(a("s6", 0, 20), a("hl", 0, 20), a("acc"), OP.subtract)
+            tt(a("s6", 20, 40), a("hl", 20, 40), a("acc"), OP.subtract)
         tt(a("hh", 0, C), ind(pw, a("lp1")), a("osg"), OP.mult)
+        if t == 0:
+            ts(a("li", LQ, LQ + 40), a("s6"), 0.5, OP.mult)
+        tt(a("kk", 160, C), a("q", 160, C), a("ph", 160, C), OP.min)
+        if t == 0:
+            cp(ind(a("r0"), a("lpp")), a("tab", 0, C))
         tt(a("ssw"), ind(a("hh", 0, C + 1), a("lrs")), a("wr"), OP.mult)
         if t == 0:
-            post_lists()
-            act(a("pp"), ind(pw, a("lpost")))
-        act(a("sswp"), ind(a("ssw"), a("lpost")))
-        tt(a("kk"), a("q"), P, OP.min)
-        scan(a("pre"), a("ssw"), P, 0.0, OP.add, OP.subtract)
-        tt(a("yy"), a("kk"), a("osg"), OP.add)
-        scan(a("dd", 1, C + 1), a("sswp"), a("pp"), 0.0, OP.add, OP.subtract)
-        act(a("jp"), ind(a("yy"), a("lpar")), bias=-1.0)
+            conv("cv", a("r0"))
+            ts(col(1), kf, (C - 1) / 2.0, OP.add)
+            ts(col(2), kf, -4.0 / K, OP.mult)
+            ts(col(3), kf, -1.0 / M, OP.mult, float(CC // M), OP.add)
+            ts(col(5), kf, 4.0 / K, OP.mult, 1.0, OP.add)
+            ts(a("lpost"), w16("cv"), col(0), OP.add)
+            tt(a("yy"), a("kk"), a("osg"), OP.add)
+            act(a("sswp"), ind(a("ssw"), a("lpost")))
+            act(a("jp"), ind(a("yy"), a("lpar")), bias=-1.0)
+            cp(a("pp"), ind(pw, a("lpost")))
+            conv("pcv", P, "cvp")
+            scan(a("pre"), a("ssw"), P, 0.0, OP.add, OP.subtract)
+            ts(col(6), kf, -4096.0 / K, OP.mult, 512.0, OP.add)
+            ts(col(7), kf, 4.0 / K, OP.mult, 0.75, OP.add)
+            ts(a("n1k"), a("nw"), 1.0 / 1024, OP.mult)
+            ts(a("base", 20, 40), a("base", 0, 20), kf, OP.add)
+            tt(col(4), a("pf", 5, 6), a("pf", 2, 3), OP.add)
+        else:
+            act(a("sswp"), ind(a("ssw"), a("lpost")))
+            tt(a("yy"), a("kk"), a("osg"), OP.add)
+            act(a("jp"), ind(a("yy"), a("lpar")), bias=-1.0)
+            scan(a("pre"), a("ssw"), P, 0.0, OP.add, OP.subtract)
         conv("ycv", a("yy"), "cvp")
-        conv("pcv", P, "cvp")
-        tt(a("a2"), ind(a("dd", 0, C + 1), a("lq")), a("pre"), OP.subtract)
-        conv("jcv", a("jp"), "cvp")
+        scan(a("dd", 1, C + 1), a("sswp"), a("pp"), 0.0, OP.add, OP.subtract)
         ts(a("s2"), w16("ycv"), 1.0, OP.add, col(5), OP.min)
         ts(a("kw"), w16("pcv"), col(2), OP.add)
-        tt(a("s2"), a("s2"), w16("jcv"), OP.max)
+        conv("jcv", a("jp"), "cvp")
+        tt(a("a2", 0, 160), ind(a("dd", 0, C + 1), a("li", LQ, LQ + 10)), a("pre", 0, 160), OP.subtract)
+        tt(a("s3"), a("s2"), w16("jcv"), OP.max)
+        tt(a("a2", 160, C), ind(a("dd", 0, C + 1), a("li", LQ + 10, LQ + 20)), a("pre", 160, C), OP.subtract)
+        tt(a("s4"), a("s3"), a("n1k"), OP.add)
         tt(a("kw"), a("kw"), a("szw"), OP.mult)
-        tt(a("s2"), a("s2"), a("n1k"), OP.add)
-        ts(a("lvn"), a("s2"), 1024.0, OP.mult, col(6), OP.add)
+        ts(a("s2"), a("s2"), col(7), OP.is_gt)
+        ts(a("lvn"), a("s4"), 1024.0, OP.mult, col(6), OP.add)
+        conv("cv", a("a2"))
         act(a("vn"), ind(a("cs"), a("lvn")))
         act(a("d1"), a("osg"), bias=float(M + 2), scale=2.0)
         if t == 0:
             act(a("cv4"), ind(a("blk", 16, 32), a("lpm")))
-        conv("cv", a("a2"))
+        unit(t, 0)
         tt(a("s1"), a("kw"), w16("cv"), OP.subtract)
+        tt(a("s2"), a("s2"), a("base", 0, 20), OP.mult)
         ts(a("lsig"), a("s1"), col(1), OP.add)
+        tt(a("ocw"), a("s2"), a("base", 20, 40), OP.add)
+        unit(t, 1)
         cp(ind(a("vs"), a("lsig")), a("vn"))
+        unit(t, 2)
         act(a("ua"), a("vs"), AF.Abs)
         act(a("sg", 0, C), a("vs"), AF.Sign)
         ts(a("cc", 0, C), a("vs"), 0.0, OP.is_lt, 2 * SC, OP.max)
+        unit(t, 3)
         scan(a("ff"), a("cc", 0, C), a("vs"), 1.0, OP.add, OP.min)
         act(a("fn"), ind(a("ff"), a("lsig")), scale=1 / SC)
         tt(a("vbk"), a("ua"), a("sg", 1, C + 1), OP.mult)
@@ -358,37 +386,41 @@ def rank_program(g, core, T, topo):
              OP.add, OP.subtract)
         conv("cv", a("fn"))
         conv("cvb", a("gn"))
+        rn(0, 112)
         tt(a("ri"), w16("cv"), w16("cvb"), OP.min)
         tt(a("si"), w16("cv"), w16("cvb"), OP.add)
-        ts(a("rl"), a("ri"), M - 1, OP.bitwise_and)
-        ts(a("sl"), a("si"), M - 1, OP.bitwise_and, 1, OP.arith_shift_right)
-        ts(a("npb"), a("rl"), 2.5, OP.is_lt, float(C), OP.mult)
+        rn(112, 192)
+        tt(a("npb"), a("ri"), a("ocw"), OP.is_equal)
+        ts(a("sl"), a("si"), M - 1, OP.bitwise_and)
         ts(a("lb"), a("ri"), 1.0 / M, OP.mult, col(3), OP.add)
-        tt(a("lv", 0, 20), a("npb"), a("sl"), OP.min)
-        tt(a("lv", 20, 40), a("npb"), a("nw"), OP.add)
-        cp(a("llv"), a("lv"))
-        ts(a("lenr"), ind(a("tab"), a("llv", 0, 20)), 2.0, OP.mult)
+        tt(a("lv", 0, 20), a("npb"), a("sl"), OP.mult)
+        ts(a("s2"), a("npb"), float(C), OP.mult)
+        cp(a("llv", 0, 20), a("lv", 0, 20))
+        tt(a("lv", 20, 40), a("s2"), a("nw"), OP.add)
+        rn(192, 256)
+        cp(a("lenr"), ind(a("tab"), a("llv", 0, 20)))
+        cp(a("llv", 20, 40), a("lv", 20, 40))
+        rn(256, C)
         act(a("vf"), ind(a("tab"), a("llv", 20, 40)))
-        if t == 0:
-            for b in range(4):
-                s = 2 - 2 * (b // 2)
-                quant("qe", "se", 128 * b, 128 * b + 128, a("e%d" % (b % 2), s, s + 512))
         for b in range(4):
             mm(4 + b, "qe", "se", 128 * b, "lc%d" % t, "ls%d" % t, 0, C)
         for b in range(4):
             act(a("db", b, 4 * C, 4), bank(4 + b, C))
         dma("y", T.db[:, 4 * C:8 * C], T.db[:, 0:4 * C], [a("db", 4 * C, 8 * C)], [a("db", 0, 4 * C)])
         scan(a("tt", 2 * C + 1, 3 * C + 1), a("lenr"), a("d1"), float(CC // 2 - 1), OP.add, OP.subtract)
-        cp(a("tg"), ind(a("tt"), a("lb")))
+        tt(a("tg"), ind(a("tt"), a("lb")), a("rn"), OP.add)
         conv("cv", a("tg"))
-        tt(a("s1"), w16("cv"), a("ri"), OP.add)
-        ts(a("lpos"), a("s1"), 0.5, OP.mult, col(0), OP.add)
+        ts(a("lpos"), w16("cv"), col(0), OP.add, 0.5, OP.mult)
         cp(ind(a("orow"), a("lpos")), a("vf"))
         conv("cv", a("orow", 0, 136), "cv4", 0, 136)
         conv("cvb", a("orow", A, C), "cv4", A, C)
         ts(a(lo, 0, 34), a("cv", 3, 136, 4), 4.0, OP.mult, col(4), OP.add)
         send(t, a(lo, 0, 34), a(ll)[0], "la%d" % t)
         ts(a(lo, 48, 96), a("cvb", A + 3, C, 4), 4.0, OP.mult, col(4), OP.add)
+        if last:
+            ts(a("tg"), a("orow"), float(C), OP.is_ge, -float(C), OP.mult)
+        if t == 0:
+            quant("qv", "sv", 0, 128, a("vb"))
         wa, wb = a("xb", 0, 8 * C), a("xb", 4 * C, 12 * C)
         for c0, c1 in ((0, 10), (10, 30), (30, 48)):
             act(a("g2o", 16 * c0, 16 * c1), ind(wb, a(lo, 48 + c0, 48 + c1)))
@@ -400,9 +432,8 @@ def rank_program(g, core, T, topo):
         for b in range(4):
             mm(b, "qw", "sw", 128 * b, "qz", "zs", A, C)
         if last:
-            ts(a("ot1"), a("orow"), float(C), OP.is_ge, -float(C), OP.mult)
-        if t == 0:
-            quant("qv", "sv", 0, 128, a("vb"))
+            tt(a("lenr"), a("tg"), a("orow"), OP.add)
+            dma("y", T.ot[:], T.lenr[0:128:16, :], [], [a("lenr")])
         da, dbb = a("db", 0, 8 * C), a("db", 4 * C, 12 * C)
         for c0, c1 in ((0, 10), (10, 33)):
             act(a("g2a", 16 * c0, 16 * c1), ind(dbb, a(ll, c0, c1)))
@@ -411,26 +442,24 @@ def rank_program(g, core, T, topo):
         qn, sn = "qx%d" % (t + 1), "sx%d" % (t + 1)
         lq, ls = ("qv", "sv") if last else ("qu2", "su2")
         ts(a("xb", 4 * A, 4 * C), a("x128", 4 * A, 4 * C), 0.0078125, OP.mult)
-        quant(qn, sn, A, C, a("xb", 4 * A, 4 * C))
-        mm(0, lq, ls, 0, qn, sn, A, C)
-        if last:
-            dma("y", T.oc[:, 4 * A:4 * C], u8(a(qn, A, C)), [], [a(qn, A, C)])
         for c0, c1 in ((0, 8), (8, 32)):
             e0, e1 = 16 * c0, 16 * c1
             tt(a("z", e0, e1), ind(da, a(ll, c0, c1)), a("g2a", e0 + 4, e1 + 4), OP.subtract)
             act(a("z128", e0, e1), a("z", e0, e1), scale=128.0)
+        quant(qn, sn, A, C, a("xb", 4 * A, 4 * C))
+        if last:
+            dma("y", T.oc[:, 4 * A:4 * C], u8(a(qn, A, C)), [], [a(qn, A, C)])
         quant("qz", "zs", 0, A, a("z", 0, 4 * A))
         for b in range(4):
             mm(4 + b, "qw", "sw", 128 * b, "qz", "zs", 0, A)
+        mm(0, lq, ls, 0, qn, sn, A, C)
         if last:
             act(a("ys", A, C), bank(0, C - A))
             dma("s", T.y[:, A:C], T.ys[:, A:C], [], [a("ys", A, C)])
-            tt(a("ot2"), a("ot1"), a("orow"), OP.add)
-            dma("y", T.ot[:], T.ot2[0:128:16, :], [], [a("ot2")])
-        else:
-            defects(A, C, 0)
         for b in range(4):
             tt(a("x128", b, 4 * A, 4), bank(4 + b, A), a("z128", b, 4 * A, 4), OP.add)
+        if not last:
+            defects(A, C, 0)
         ts(a("xb", 0, 4 * A), a("x128", 0, 4 * A), 0.0078125, OP.mult)
         quant(qn, sn, 0, A, a("xb", 0, 4 * A))
         mm(1, lq, ls, 0, qn, sn, 0, A)

@@ -5,22 +5,24 @@ STEP = [1, 2, 3]
 M = 2048
 CC = 2 * 640 * M
 K = float(2 ** 22)
+KH = 640.0 / K
 BIG = float(2 ** 24)
 SC = 2.0 ** -23
 F32, BF, I32, U16, Q4, U8 = "float32", "bfloat16", "int32", "uint16", "float8_e4m3fn_x4", "uint8"
 LISTS = ["lpm", "lend", "lpar", "lp1", "lrs", "ldr", "lq", "lpp", "lpost", "lsig", "lb", "lpos", "lvn"]
-LQ = 20 * LISTS.index("lq")
+LQ, LS = 20 * LISTS.index("lq"), 20 * LISTS.index("lsig")
 
 SCRATCH = {"ps": ("psum", [128, 4096], F32)}
 for _d, _l in (
     (BF, "xb:3840 db:3840 x128:1280 z:1280 z128:1280 g2o:784 g2a:528 ub:512 vb:512 ones:516 e0:516 e1:516 junk:3360 "
-         "cvp m2 q p:336 ph:336 pp osg hh:336 pcv kk yy jp ycv jcv sg:336"),
-    (Q4, "qz qu:128 qu2:128 qv:128 qw:512 qe:512 qx0 qx1 qx2 qx3 lc0 lc1 lc2"),
-    (U8, "zs su:128 su2:128 sv:128 sw:512 se:512 sx0 sx1 sx2 sx3 ls0 ls1 ls2"),
-    (I32, "szw:20 prw:20 ip:4 pi:8 mi:32 mj:32 ri:20 si:20 sl:20"),
+         "cvp m2 q p:336 ph:336 pp osg:336 pcv kk yy jp ycv jcv sg:336"),
+    ("float16", "a2 cvh cvo"),
+    (Q4, "qz qy:128 qu:128 qu2:128 qv:128 qw:512 qe:512 qx0 qx1 qx2 qx3 lc0 lc1 lc2"),
+    (U8, "zs ys2:128 su:128 su2:128 sv:128 sw:512 se:512 sx0 sx1 sx2 sx3 ls0 ls1 ls2"),
+    (I32, "szw:20 prw:20 pi:8 mi:32 mj:32 ri:20 si:20 sl:20"),
     (U16, "li:%d llv:40 lu:8 ll0:34 ll1:34 ll2:34 lo0:96 lo1:96 lo2:96" % (20 * len(LISTS))),
-    (F32, "pf:8 col:16 i16:20 ii:16 nw:20 nb:20 n1k:20 ba:32 bb:32 blk:32 cv16 cv4 tab:648 cs:1856 c2 tt:968 endw:20 "
-          "s1:20 s2:20 s3:20 s4:20 s6:40 hl:40 acc:20 base:40 ocw:20 endr wr r0 cv cvb ssw sswp pre dd:328 a2 kw:20 "
+    (F32, "pf:8 col:16 i16:20 ii:16 nw:20 nb:20 ba:64 blk:32 cv16 cv4 tab:648 cs:1856 c2 tt:968 "
+          "s1:20 s2:20 s3:20 s4:20 s6:40 hl:60 acc:20 base:60 ocw:20 endr wr r0 cv cvb hh ssw sswp pre dd:328 kw:20 "
           "vn vs cc:328 ua vbk ff gg fn gn rn d1 npb:20 lv:40 lenr vf tg orow ys"),
 ):
     for _e in _l.split():
@@ -208,21 +210,26 @@ def rank_program(g, core, T, topo):
     dma("y", T.sw[:], T.ws[:], [a("sw")], [])
     dma("y", T.vb[:], T.v[:], [a("vb")], [])
 
-    iota(a("ip", 0, 1), [[0, 1]], 0, 1, small=False)
+    ip, endw, n1k, osg = a("pi", 4, 5), a("hl", 40, 60), a("base", 40, 60), a("osg", 0, C)
+    iota(ip, [[0, 1]], 0, 1, small=False)
     iota(a("i16"), [[16, 20]], 0, 0)
     iota(a("ii"), [[1, 16]], 16, 0)
     iota(a("tab"), [[1, 648]], 0, 0)
+    iota(a("ones"), [[0, 516]], 1, 0)
+    for k in range(2):
+        o = a("e%d" % k)
+        run("g", lambda: g.affine_select(o[0], T.ones[:], [[1, 516]], OP.is_equal, 0.0, -2 - k, -4), [o], [a("ones")])
     ms(a("m2"), -2.0)
     ms(a("p", 0, 1), 2.0)
     ms(a("ph", 0, 1), 0.5)
     ms(a("dd", 0, 1), 0.0)
     ms(a("sg", C, C + 1), -1.0)
-    ms(a("hh", C, C + 1), 1.0)
+    ms(a("osg", C, C + 1), 1.0)
     ms(a("cc", C, C + 1), 1.0)
     ms(a("g2o", 768, 784), 0.0)
-    ts(a("pi", 0, 1), a("ip", 0, 1), 15, OP.bitwise_and)
-    ts(a("pi", 1, 2), a("ip", 0, 1), 2, OP.arith_shift_right, 3, OP.bitwise_and)
-    ts(a("pi", 2, 3), a("ip", 0, 1), 3, OP.bitwise_and)
+    ts(a("pi", 0, 1), ip, 15, OP.bitwise_and)
+    ts(a("pi", 1, 2), ip, 2, OP.arith_shift_right, 3, OP.bitwise_and)
+    ts(a("pi", 2, 3), ip, 3, OP.bitwise_and)
     cp(a("lu"), a("i16", 0, 8))
     cp(a("pf", 0, 3), a("pi", 0, 3))
     ts(a("nw"), a("i16"), a("pf", 0, 1), OP.add)
@@ -238,13 +245,13 @@ def rank_program(g, core, T, topo):
     ts(a("hl", 0, 20), a("i16"), 16.0, OP.add)
     ts(a("base", 0, 20), a("nw"), float(M), OP.mult, 1.0 - CC // 2, OP.add)
     kf = a("pf", 4, 5)
-    tt(a("endw"), a("nw"), a("szw"), OP.add)
-    ts(a("ba"), a("mj"), 0.0, OP.is_equal, -BIG, OP.mult)
-    ts(a("bb"), a("mj"), 1.0, OP.is_equal, K, OP.mult)
+    tt(endw, a("nw"), a("szw"), OP.add)
+    ts(a("ba", 0, 32), a("mj"), 0.0, OP.is_equal, -BIG, OP.mult)
+    ts(a("ba", 32, 64), a("mj"), 1.0, OP.is_equal, K, OP.mult)
     ts(col(0), kf, -1.0, OP.mult)
-    cp(a("lend"), a("endw"))
+    cp(a("lend"), endw)
     tt(a("s1"), a("nw"), a("prw"), OP.subtract)
-    tt(a("blk"), a("ba"), a("bb"), OP.add)
+    tt(a("blk"), a("ba", 0, 32), a("ba", 32, 64), OP.add)
     cp(a("lpar"), a("prw"))
     cp(a("endr"), ind(a("tab"), a("lend")))
     off = 0
@@ -254,10 +261,11 @@ def rank_program(g, core, T, topo):
         off += n
     act(a("cv16"), ind(a("blk", 0, 16), a("lpm")))
     act(a("cvp"), a("cv16"), scale=4.0 / K)
+    act(a("cvh"), a("cv16"), scale=KH)
     for e, n, f in ((0, 512, -0.5), (512, 512, -0.5), (1024, 512, 0.5), (1536, C, 1.0)):
         act(a("cs", e, e + n), a("tab", 0, n), bias=f * (2 - CC) * SC, scale=f * 2 * M * SC)
     ts(a("s2"), a("s1"), 1.0, OP.is_gt)
-    tt(a("s4"), a("s1"), a("endw"), OP.add)
+    tt(a("s4"), a("s1"), endw, OP.add)
     quant("qu", "su", 0, 128, a("ub"))
     ts(a("ldr"), a("s4"), -1.0, OP.add)
     ts(a("lp1"), a("prw"), 1.0, OP.add)
@@ -267,7 +275,7 @@ def rank_program(g, core, T, topo):
                                           T.qu[:, 0:128].bitcast(dt.uint32).indirect(lu[0])),
         [a("qu2")], [a("qu"), lu])
     run("v", lambda: g.vector.tensor_copy(T.su2[:, 0:128], T.su[:, 0:128].indirect(lu[0])), [a("su2")], [a("su"), lu])
-    tt(a("s4"), a("endw"), a("s3"), OP.subtract)
+    tt(a("s4"), endw, a("s3"), OP.subtract)
     quant("qx0", "sx0", 0, C, a("xb", 0, 4 * C))
     cp(a("lrs"), a("s4"))
 
@@ -292,10 +300,6 @@ def rank_program(g, core, T, topo):
     cp(a("r0"), ind(a("tab"), a("ldr")))
     tt(a("hl", 20, 40), a("hl", 0, 20), a("s6", 0, 20), OP.add)
     defects(0, C, 0)
-    iota(a("ones"), [[0, 516]], 1, 0)
-    for k in range(2):
-        o = a("e%d" % k)
-        run("g", lambda: g.affine_select(o[0], T.ones[:], [[1, 516]], OP.is_equal, 0.0, -2 - k, -4), [o], [a("ones")])
     iota(a("c2"), [[0, C]], M * 2 - 1, 0)
     iota(a("tt"), [[0, 968]], CC // 2 - 1, 0)
     iota(a("db", 8 * C, 12 * C), [[0, 4 * C]], 0, 0)
@@ -310,64 +314,69 @@ def rank_program(g, core, T, topo):
         pw = a("ph", 0, C + 1)
         if t:
             act(a("pp"), ind(pw, a("lpost")))
-            conv("pcv", P, "cvp")
         else:
             tt(a("wr"), ind(a("endr"), a("lpar")), a("r0"), OP.subtract)
-        tt(a("osg"), ind(pw, a("lend")), a("p", 0, C), OP.mult)
-        tt(a("kk", 0, 160), a("q", 0, 160), a("ph", 0, 160), OP.min)
+        tt(a("kk"), a("q"), P, OP.min)
+        tt(osg, ind(pw, a("lend")), a("p", 0, C), OP.mult)
         if t == 0:
             tt(a("s6", 0, 20), a("hl", 0, 20), a("acc"), OP.subtract)
             tt(a("s6", 20, 40), a("hl", 20, 40), a("acc"), OP.subtract)
-        tt(a("hh", 0, C), ind(pw, a("lp1")), a("osg"), OP.mult)
-        if t == 0:
+            tt(a("yy"), a("kk"), osg, OP.add)
             ts(a("li", LQ, LQ + 40), a("s6"), 0.5, OP.mult)
-        tt(a("kk", 160, C), a("q", 160, C), a("ph", 160, C), OP.min)
-        if t == 0:
-            cp(ind(a("r0"), a("lpp")), a("tab", 0, C))
-        tt(a("ssw"), ind(a("hh", 0, C + 1), a("lrs")), a("wr"), OP.mult)
-        if t == 0:
-            conv("cv", a("r0"))
-            ts(col(1), kf, (C - 1) / 2.0, OP.add)
+            act(a("jp"), ind(a("yy"), a("lpar")), bias=-1.0)
+            ts(col(1), kf, KH, OP.mult, (C - 1) / 2.0, OP.add)
             ts(col(2), kf, -4.0 / K, OP.mult)
             ts(col(3), kf, -1.0 / M, OP.mult, float(CC // M), OP.add)
             ts(col(5), kf, 4.0 / K, OP.mult, 1.0, OP.add)
+            cp(ind(a("r0"), a("lpp")), a("tab", 0, C))
+            tt(a("hh"), ind(pw, a("lp1")), a("wr"), OP.mult)
+            conv("cv", a("r0"))
+            tt(a("ssw"), ind(a("osg", 0, C + 1), a("lrs")), a("hh"), OP.mult)
             ts(a("lpost"), w16("cv"), col(0), OP.add)
-            tt(a("yy"), a("kk"), a("osg"), OP.add)
-            act(a("sswp"), ind(a("ssw"), a("lpost")))
-            act(a("jp"), ind(a("yy"), a("lpar")), bias=-1.0)
-            cp(a("pp"), ind(pw, a("lpost")))
+            conv("ycv", a("yy"), "cvp")
             conv("pcv", P, "cvp")
+            act(a("sswp"), ind(a("ssw"), a("lpost")))
+            cp(a("pp"), ind(pw, a("lpost")))
             scan(a("pre"), a("ssw"), P, 0.0, OP.add, OP.subtract)
+            scan(a("dd", 1, C + 1), a("sswp"), a("pp"), 0.0, OP.add, OP.subtract)
+            ts(a("s2"), w16("ycv"), 1.0, OP.add, col(5), OP.min)
+            conv("jcv", a("jp"), "cvp")
+            ts(a("kw"), w16("pcv"), col(2), OP.add)
             ts(col(6), kf, -4096.0 / K, OP.mult, 512.0, OP.add)
             ts(col(7), kf, 4.0 / K, OP.mult, 0.75, OP.add)
-            ts(a("n1k"), a("nw"), 1.0 / 1024, OP.mult)
+            ts(n1k, a("nw"), 1.0 / 1024, OP.mult)
+        else:
+            tt(a("hh"), ind(pw, a("lp1")), a("wr"), OP.mult)
+            tt(a("yy"), a("kk"), osg, OP.add)
+            act(a("jp"), ind(a("yy"), a("lpar")), bias=-1.0)
+            tt(a("ssw"), ind(a("osg", 0, C + 1), a("lrs")), a("hh"), OP.mult)
+            act(a("sswp"), ind(a("ssw"), a("lpost")))
+            conv("ycv", a("yy"), "cvp")
+            conv("pcv", P, "cvp")
+            scan(a("pre"), a("ssw"), P, 0.0, OP.add, OP.subtract)
+            ts(a("s2"), w16("ycv"), 1.0, OP.add, col(5), OP.min)
+            conv("jcv", a("jp"), "cvp")
+            ts(a("kw"), w16("pcv"), col(2), OP.add)
+            scan(a("dd", 1, C + 1), a("sswp"), a("pp"), 0.0, OP.add, OP.subtract)
+        tt(a("s3"), a("s2"), w16("jcv"), OP.max)
+        tt(a("kw"), a("kw"), a("szw"), OP.mult)
+        ts(a("s6", 0, 20), a("s2"), col(7), OP.is_gt)
+        tt(a("a2", 0, 160), ind(a("dd", 0, C + 1), a("li", LQ, LQ + 10)), a("pre", 0, 160), OP.subtract)
+        tt(a("s4"), a("s3"), n1k, OP.add)
+        tt(a("a2", 160, C), ind(a("dd", 0, C + 1), a("li", LQ + 10, LQ + 20)), a("pre", 160, C), OP.subtract)
+        ts(a("lvn"), a("s4"), 1024.0, OP.mult, col(6), OP.add)
+        if t == 0:
+            ts(col(8), kf, -KH, OP.mult)
             ts(a("base", 20, 40), a("base", 0, 20), kf, OP.add)
             tt(col(4), a("pf", 5, 6), a("pf", 2, 3), OP.add)
-        else:
-            act(a("sswp"), ind(a("ssw"), a("lpost")))
-            tt(a("yy"), a("kk"), a("osg"), OP.add)
-            act(a("jp"), ind(a("yy"), a("lpar")), bias=-1.0)
-            scan(a("pre"), a("ssw"), P, 0.0, OP.add, OP.subtract)
-        conv("ycv", a("yy"), "cvp")
-        scan(a("dd", 1, C + 1), a("sswp"), a("pp"), 0.0, OP.add, OP.subtract)
-        ts(a("s2"), w16("ycv"), 1.0, OP.add, col(5), OP.min)
-        ts(a("kw"), w16("pcv"), col(2), OP.add)
-        conv("jcv", a("jp"), "cvp")
-        tt(a("a2", 0, 160), ind(a("dd", 0, C + 1), a("li", LQ, LQ + 10)), a("pre", 0, 160), OP.subtract)
-        tt(a("s3"), a("s2"), w16("jcv"), OP.max)
-        tt(a("a2", 160, C), ind(a("dd", 0, C + 1), a("li", LQ + 10, LQ + 20)), a("pre", 160, C), OP.subtract)
-        tt(a("s4"), a("s3"), a("n1k"), OP.add)
-        tt(a("kw"), a("kw"), a("szw"), OP.mult)
-        ts(a("s2"), a("s2"), col(7), OP.is_gt)
-        ts(a("lvn"), a("s4"), 1024.0, OP.mult, col(6), OP.add)
-        conv("cv", a("a2"))
+        conv("cvo", a("a2"), "cvh")
         act(a("vn"), ind(a("cs"), a("lvn")))
-        act(a("d1"), a("osg"), bias=float(M + 2), scale=2.0)
+        act(a("d1"), osg, bias=float(M + 2), scale=2.0)
         if t == 0:
             act(a("cv4"), ind(a("blk", 16, 32), a("lpm")))
         unit(t, 0)
-        tt(a("s1"), a("kw"), w16("cv"), OP.subtract)
-        tt(a("s2"), a("s2"), a("base", 0, 20), OP.mult)
+        tt(a("s1"), a("kw"), w16("cvo"), OP.subtract)
+        tt(a("s2"), a("s6", 0, 20), a("base", 0, 20), OP.mult)
         ts(a("lsig"), a("s1"), col(1), OP.add)
         tt(a("ocw"), a("s2"), a("base", 20, 40), OP.add)
         unit(t, 1)
@@ -380,11 +389,12 @@ def rank_program(g, core, T, topo):
         scan(a("ff"), a("cc", 0, C), a("vs"), 1.0, OP.add, OP.min)
         act(a("fn"), ind(a("ff"), a("lsig")), scale=1 / SC)
         tt(a("vbk"), a("ua"), a("sg", 1, C + 1), OP.mult)
-        scan(a("gg", rev=True), a("cc", 1, C + 1, rev=True), a("vbk", rev=True), 1.0, OP.add, OP.min)
-        act(a("gn"), ind(a("gg"), a("lsig")), scale=1 / SC)
-        scan(a("tt", 0, 2 * C, 2, rev=True), a("c2"), a("osg", rev=True), float(2 * C - 2 * M * C - 2 + CC),
+        scan(a("tt", 0, 2 * C, 2, rev=True), a("c2"), a("osg", 0, C, rev=True), float(2 * C - 2 * M * C - 2 + CC),
              OP.add, OP.subtract)
+        scan(a("gg", rev=True), a("cc", 1, C + 1, rev=True), a("vbk", rev=True), 1.0, OP.add, OP.min)
+        act(a("gn", 0, 192), ind(a("gg"), a("li", LS, LS + 12)), scale=1 / SC)
         conv("cv", a("fn"))
+        ts(a("gn", 192, C), ind(a("gg"), a("li", LS + 12, LS + 20)), 1 / SC, OP.mult)
         conv("cvb", a("gn"))
         rn(0, 112)
         tt(a("ri"), w16("cv"), w16("cvb"), OP.min)
@@ -398,7 +408,8 @@ def rank_program(g, core, T, topo):
         cp(a("llv", 0, 20), a("lv", 0, 20))
         tt(a("lv", 20, 40), a("s2"), a("nw"), OP.add)
         rn(192, 256)
-        cp(a("lenr"), ind(a("tab"), a("llv", 0, 20)))
+        act(a("lenr", 160, C), ind(a("tab"), a("llv", 10, 20)))
+        cp(a("lenr", 0, 160), ind(a("tab"), a("llv", 0, 10)))
         cp(a("llv", 20, 40), a("lv", 20, 40))
         rn(256, C)
         act(a("vf"), ind(a("tab"), a("llv", 20, 40)))
@@ -408,9 +419,9 @@ def rank_program(g, core, T, topo):
             act(a("db", b, 4 * C, 4), bank(4 + b, C))
         dma("y", T.db[:, 4 * C:8 * C], T.db[:, 0:4 * C], [a("db", 4 * C, 8 * C)], [a("db", 0, 4 * C)])
         scan(a("tt", 2 * C + 1, 3 * C + 1), a("lenr"), a("d1"), float(CC // 2 - 1), OP.add, OP.subtract)
-        tt(a("tg"), ind(a("tt"), a("lb")), a("rn"), OP.add)
-        conv("cv", a("tg"))
-        ts(a("lpos"), w16("cv"), col(0), OP.add, 0.5, OP.mult)
+        tt(a("a2"), ind(a("tt"), a("lb")), a("rn"), OP.add)
+        conv("cvo", a("a2"), "cvh")
+        ts(a("lpos"), w16("cvo"), col(8), OP.add, 0.5, OP.mult)
         cp(ind(a("orow"), a("lpos")), a("vf"))
         conv("cv", a("orow", 0, 136), "cv4", 0, 136)
         conv("cvb", a("orow", A, C), "cv4", A, C)
@@ -422,15 +433,18 @@ def rank_program(g, core, T, topo):
         if t == 0:
             quant("qv", "sv", 0, 128, a("vb"))
         wa, wb = a("xb", 0, 8 * C), a("xb", 4 * C, 12 * C)
-        for c0, c1 in ((0, 10), (10, 30), (30, 48)):
+        for c0, c1 in ((0, 12), (12, 34), (34, 48)):
             act(a("g2o", 16 * c0, 16 * c1), ind(wb, a(lo, 48 + c0, 48 + c1)))
-        for c0, c1 in ((0, 8), (8, 28), (28, 48)):
+        for c0, c1 in ((0, 10), (10, 32), (32, 48)):
             e0, e1 = 4 * A + 16 * c0, 4 * A + 16 * c1
             tt(a("z", e0, e1), ind(wa, a(lo, 48 + c0, 48 + c1)), a("g2o", 16 * c0 + 4, 16 * c1 + 4), OP.subtract)
             act(a("z128", e0, e1), a("z", e0, e1), scale=128.0)
-        quant("qz", "zs", A, C, a("z", 4 * A, 4 * C))
+        quant("qz", "zs", A, 2 * A, a("z", 4 * A, 8 * A))
+        quant("qy", "ys2", 0, A, a("z", 4 * (C - A), 4 * C))
         for b in range(4):
-            mm(b, "qw", "sw", 128 * b, "qz", "zs", A, C)
+            mm(b, "qw", "sw", 128 * b, "qz", "zs", A, 2 * A)
+        for b in range(4):
+            mm(4 + b, "qw", "sw", 128 * b, "qy", "ys2", 0, A)
         if last:
             tt(a("lenr"), a("tg"), a("orow"), OP.add)
             dma("y", T.ot[:], T.lenr[0:128:16, :], [], [a("lenr")])
@@ -438,10 +452,14 @@ def rank_program(g, core, T, topo):
         for c0, c1 in ((0, 10), (10, 33)):
             act(a("g2a", 16 * c0, 16 * c1), ind(dbb, a(ll, c0, c1)))
         for b in range(4):
-            tt(a("x128", 4 * A + b, 4 * C, 4), bank(b, C - A), a("z128", 4 * A + b, 4 * C, 4), OP.add)
+            tt(a("x128", 4 * A + b, 8 * A, 4), bank(b, A), a("z128", 4 * A + b, 8 * A, 4), OP.add)
+        for b in range(4):
+            e0 = 512 * (4 + b)
+            tt(a("x128", 8 * A + b, 4 * C, 4), a("ps", e0 + 3 * A - C, e0 + A), a("z128", 8 * A + b, 4 * C, 4), OP.add)
         qn, sn = "qx%d" % (t + 1), "sx%d" % (t + 1)
         lq, ls = ("qv", "sv") if last else ("qu2", "su2")
-        ts(a("xb", 4 * A, 4 * C), a("x128", 4 * A, 4 * C), 0.0078125, OP.mult)
+        ts(a("xb", 4 * A, 8 * A), a("x128", 4 * A, 8 * A), 0.0078125, OP.mult)
+        ts(a("xb", 8 * A, 4 * C), a("x128", 8 * A, 4 * C), 0.0078125, OP.mult)
         for c0, c1 in ((0, 8), (8, 32)):
             e0, e1 = 16 * c0, 16 * c1
             tt(a("z", e0, e1), ind(da, a(ll, c0, c1)), a("g2a", e0 + 4, e1 + 4), OP.subtract)
@@ -451,20 +469,20 @@ def rank_program(g, core, T, topo):
             dma("y", T.oc[:, 4 * A:4 * C], u8(a(qn, A, C)), [], [a(qn, A, C)])
         quant("qz", "zs", 0, A, a("z", 0, 4 * A))
         for b in range(4):
-            mm(4 + b, "qw", "sw", 128 * b, "qz", "zs", 0, A)
-        mm(0, lq, ls, 0, qn, sn, A, C)
+            mm(b, "qw", "sw", 128 * b, "qz", "zs", 0, A)
+        mm(4, lq, ls, 0, qn, sn, A, C)
         if last:
-            act(a("ys", A, C), bank(0, C - A))
+            act(a("ys", A, C), bank(4, C - A))
             dma("s", T.y[:, A:C], T.ys[:, A:C], [], [a("ys", A, C)])
         for b in range(4):
-            tt(a("x128", b, 4 * A, 4), bank(4 + b, A), a("z128", b, 4 * A, 4), OP.add)
+            tt(a("x128", b, 4 * A, 4), bank(b, A), a("z128", b, 4 * A, 4), OP.add)
         if not last:
-            defects(A, C, 0)
+            defects(A, C, 4)
         ts(a("xb", 0, 4 * A), a("x128", 0, 4 * A), 0.0078125, OP.mult)
         quant(qn, sn, 0, A, a("xb", 0, 4 * A))
-        mm(1, lq, ls, 0, qn, sn, 0, A)
+        mm(5, lq, ls, 0, qn, sn, 0, A)
         if last:
-            cp(a("ys", 0, A), bank(1, A))
+            cp(a("ys", 0, A), bank(5, A))
             dma("y", T.oc[:, 0:4 * A], u8(a(qn, 0, A)), [], [a(qn, 0, A)])
             for k in range(4):
                 dma("ys"[k % 2], T.osc[4 * k:4 * k + 4, :], T[sn][32 * k:32 * k + 4, :], [], [a(sn)])
@@ -472,7 +490,7 @@ def rank_program(g, core, T, topo):
         else:
             spread(t + 1)
             dma("y", T.xb[:, 4 * C:8 * C], T.xb[:, 0:4 * C], [a("xb", 4 * C, 8 * C)], [a("xb", 0, 4 * C)])
-            defects(0, A, 1)
+            defects(0, A, 5)
 
     for s, n in count.items():
         g.wait_ge(T.sem[s], n)

@@ -10,20 +10,20 @@ BIG = float(2 ** 24)
 SC = 2.0 ** -23
 F32, BF, I32, U16, Q4, U8 = "float32", "bfloat16", "int32", "uint16", "float8_e4m3fn_x4", "uint8"
 LISTS = ["lpm", "lend", "lpar", "lp1", "lrs", "ldr", "lq", "lpp", "lpost", "lsig", "lb", "lpos", "lvn"]
-LQ, LS = 20 * LISTS.index("lq"), 20 * LISTS.index("lsig")
+LQ = 20 * LISTS.index("lq")
 
 SCRATCH = {"ps": ("psum", [128, 4096], F32)}
 for _d, _l in (
     (BF, "xb:3840 db:3840 x128:1280 z:1280 z128:1280 g2o:784 g2a:528 ub:512 vb:512 ones:516 e0:516 e1:516 junk:3360 "
-         "cvp m2 q p:336 ph:336 pp osg:336 pcv kk yy jp ycv jcv sg:336"),
-    ("float16", "a2 cvh cvo"),
+         "cvp m2 q p:336 ph:336 pp osg:336 pcv kk yy jp ycv jcv sg:336 mk:336 npr"),
+    ("float16", "a2 cvh cvo cf lenn lenb"),
     (Q4, "qz qy:128 qu:128 qu2:128 qv:128 qw:512 qe:512 qx0 qx1 qx2 qx3 lc0 lc1 lc2"),
     (U8, "zs ys2:128 su:128 su2:128 sv:128 sw:512 se:512 sx0 sx1 sx2 sx3 ls0 ls1 ls2"),
-    (I32, "szw:20 prw:20 pi:8 mi:32 mj:32 ri:20 si:20 sl:20"),
-    (U16, "li:%d llv:40 lu:8 ll0:34 ll1:34 ll2:34 lo0:96 lo1:96 lo2:96" % (20 * len(LISTS))),
+    (I32, "szw:20 prw:20 pi:8 mi:32 mj:32"),
+    (U16, "li:%d lu:8 ll0:34 ll1:34 ll2:34 lo0:96 lo1:96 lo2:96" % (20 * len(LISTS))),
     (F32, "pf:8 col:16 i16:20 ii:16 nw:20 nb:20 ba:64 blk:32 cv16 cv4 tab:648 cs:1856 c2 tt:968 "
-          "s1:20 s2:20 s3:20 s4:20 s6:40 hl:60 acc:20 base:60 ocw:20 endr wr r0 cv cvb hh ssw sswp pre dd:328 kw:20 "
-          "vn vs cc:328 ua vbk ff gg fn gn rn d1 npb:20 lv:40 lenr vf tg orow ys"),
+          "s1:20 s2:20 s3:20 s4:20 s6:40 hl:60 acc:20 n1k:20 cvs endr wr r0 cv cvb hh ssw sswp pre dd:328 kw:20 "
+          "vn vs cc:328 ua vbk ff gg fn gn rn d1 lenr vf tg orow ys"),
 ):
     for _e in _l.split():
         SCRATCH[_e.split(":")[0]] = ("sbuf", [128, int(_e.split(":")[1]) if ":" in _e else C], _d)
@@ -210,7 +210,7 @@ def rank_program(g, core, T, topo):
     dma("y", T.sw[:], T.ws[:], [a("sw")], [])
     dma("y", T.vb[:], T.v[:], [a("vb")], [])
 
-    ip, endw, n1k, osg = a("pi", 4, 5), a("hl", 40, 60), a("base", 40, 60), a("osg", 0, C)
+    ip, endw, n1k, osg = a("pi", 4, 5), a("hl", 40, 60), a("n1k"), a("osg", 0, C)
     iota(ip, [[0, 1]], 0, 1, small=False)
     iota(a("i16"), [[16, 20]], 0, 0)
     iota(a("ii"), [[1, 16]], 16, 0)
@@ -225,6 +225,7 @@ def rank_program(g, core, T, topo):
     ms(a("dd", 0, 1), 0.0)
     ms(a("sg", C, C + 1), -1.0)
     ms(a("osg", C, C + 1), 1.0)
+    ms(a("mk", C, C + 1), 0.0)
     ms(a("cc", C, C + 1), 1.0)
     ms(a("g2o", 768, 784), 0.0)
     ts(a("pi", 0, 1), ip, 15, OP.bitwise_and)
@@ -243,7 +244,6 @@ def rank_program(g, core, T, topo):
     ts(a("mj", 16, 32), a("mi", 16, 32), 3, OP.bitwise_and)
     ts(a("nb"), a("nb"), -0.5, OP.add)
     ts(a("hl", 0, 20), a("i16"), 16.0, OP.add)
-    ts(a("base", 0, 20), a("nw"), float(M), OP.mult, 1.0 - CC // 2, OP.add)
     kf = a("pf", 4, 5)
     tt(endw, a("nw"), a("szw"), OP.add)
     ts(a("ba", 0, 32), a("mj"), 0.0, OP.is_equal, -BIG, OP.mult)
@@ -291,8 +291,11 @@ def rank_program(g, core, T, topo):
             s = 2 - 2 * (b // 2)
             quant("qe", "se", 128 * b, 128 * b + 128, a("e%d" % (b % 2), s, s + 512))
 
-    def rn(lo, hi):
-        tt(a("rn", lo, hi), a("fn", lo, hi), a("gn", lo, hi), OP.min)
+    def value(lo, hi):
+        tt(a("vf", lo, hi), a("lenr", lo, hi), a("tab", lo, hi), OP.add)
+
+    def rescale(lo, hi):
+        ts(a("xb", 4 * lo, 4 * hi), a("x128", 4 * lo, 4 * hi), 0.0078125, OP.mult)
 
     mm(0, "qu2", "su2", 0, "qx0", "sx0", 0, C)
     spread(0)
@@ -343,7 +346,6 @@ def rank_program(g, core, T, topo):
             conv("jcv", a("jp"), "cvp")
             ts(a("kw"), w16("pcv"), col(2), OP.add)
             ts(col(6), kf, -4096.0 / K, OP.mult, 512.0, OP.add)
-            ts(col(7), kf, 4.0 / K, OP.mult, 0.75, OP.add)
             ts(n1k, a("nw"), 1.0 / 1024, OP.mult)
         else:
             tt(a("hh"), ind(pw, a("lp1")), a("wr"), OP.mult)
@@ -360,67 +362,60 @@ def rank_program(g, core, T, topo):
             scan(a("dd", 1, C + 1), a("sswp"), a("pp"), 0.0, OP.add, OP.subtract)
         tt(a("s3"), a("s2"), w16("jcv"), OP.max)
         tt(a("kw"), a("kw"), a("szw"), OP.mult)
-        ts(a("s6", 0, 20), a("s2"), col(7), OP.is_gt)
         tt(a("a2", 0, 160), ind(a("dd", 0, C + 1), a("li", LQ, LQ + 10)), a("pre", 0, 160), OP.subtract)
         tt(a("s4"), a("s3"), n1k, OP.add)
         tt(a("a2", 160, C), ind(a("dd", 0, C + 1), a("li", LQ + 10, LQ + 20)), a("pre", 160, C), OP.subtract)
         ts(a("lvn"), a("s4"), 1024.0, OP.mult, col(6), OP.add)
         if t == 0:
             ts(col(8), kf, -KH, OP.mult)
-            ts(a("base", 20, 40), a("base", 0, 20), kf, OP.add)
             tt(col(4), a("pf", 5, 6), a("pf", 2, 3), OP.add)
         conv("cvo", a("a2"), "cvh")
         act(a("vn"), ind(a("cs"), a("lvn")))
-        act(a("d1"), osg, bias=float(M + 2), scale=2.0)
-        if t == 0:
-            act(a("cv4"), ind(a("blk", 16, 32), a("lpm")))
+        act(a("sswp"), a("vn"), AF.Abs)
+        act(a("hh"), a("sswp"), scale=-1.0)
         unit(t, 0)
         tt(a("s1"), a("kw"), w16("cvo"), OP.subtract)
-        tt(a("s2"), a("s6", 0, 20), a("base", 0, 20), OP.mult)
-        ts(a("lsig"), a("s1"), col(1), OP.add)
-        tt(a("ocw"), a("s2"), a("base", 20, 40), OP.add)
         unit(t, 1)
-        cp(ind(a("vs"), a("lsig")), a("vn"))
+        ts(a("lsig"), a("s1"), col(1), OP.add)
         unit(t, 2)
+        cp(ind(a("vs"), a("lsig")), a("vn"))
+        unit(t, 3)
         act(a("ua"), a("vs"), AF.Abs)
         act(a("sg", 0, C), a("vs"), AF.Sign)
         ts(a("cc", 0, C), a("vs"), 0.0, OP.is_lt, 2 * SC, OP.max)
-        unit(t, 3)
         scan(a("ff"), a("cc", 0, C), a("vs"), 1.0, OP.add, OP.min)
-        act(a("fn"), ind(a("ff"), a("lsig")), scale=1 / SC)
+        act(a("mk", 0, C), a("sg", 0, C), AF.Relu)
+        act(a("fn"), ind(a("ff"), a("lsig")))
+        if t == 0:
+            act(a("cvs"), a("cv16"), scale=SC)
         tt(a("vbk"), a("ua"), a("sg", 1, C + 1), OP.mult)
+        scan(a("cf"), a("mk", 0, C), a("ones", 0, C), 0.0, OP.mult, OP.add)
+        scan(a("gg", rev=True), a("cc", 1, C + 1, rev=True), a("vbk", rev=True), 1.0, OP.add, OP.min)
+        scan(a("gn", rev=True), a("mk", 1, C + 1, rev=True), a("cf", rev=True), 0.0, OP.mult, OP.max)
+        act(a("lenn"), ind(a("gn"), a("lsig")), scale=2.0)
+        tt(a("rn"), ind(a("gg"), a("lsig")), a("fn"), OP.min)
+        act(a("d1"), osg, bias=float(M + 1))
+        act(a("tg"), a("rn"), scale=1 / SC)
         scan(a("tt", 0, 2 * C, 2, rev=True), a("c2"), a("osg", 0, C, rev=True), float(2 * C - 2 * M * C - 2 + CC),
              OP.add, OP.subtract)
-        scan(a("gg", rev=True), a("cc", 1, C + 1, rev=True), a("vbk", rev=True), 1.0, OP.add, OP.min)
-        act(a("gn", 0, 192), ind(a("gg"), a("li", LS, LS + 12)), scale=1 / SC)
-        conv("cv", a("fn"))
-        ts(a("gn", 192, C), ind(a("gg"), a("li", LS + 12, LS + 20)), 1 / SC, OP.mult)
-        conv("cvb", a("gn"))
-        rn(0, 112)
-        tt(a("ri"), w16("cv"), w16("cvb"), OP.min)
-        tt(a("si"), w16("cv"), w16("cvb"), OP.add)
-        rn(112, 192)
-        tt(a("npb"), a("ri"), a("ocw"), OP.is_equal)
-        ts(a("sl"), a("si"), M - 1, OP.bitwise_and)
-        ts(a("lb"), a("ri"), 1.0 / M, OP.mult, col(3), OP.add)
-        tt(a("lv", 0, 20), a("npb"), a("sl"), OP.mult)
-        ts(a("s2"), a("npb"), float(C), OP.mult)
-        cp(a("llv", 0, 20), a("lv", 0, 20))
-        tt(a("lv", 20, 40), a("s2"), a("nw"), OP.add)
-        rn(192, 256)
-        act(a("lenr", 160, C), ind(a("tab"), a("llv", 10, 20)))
-        cp(a("lenr", 0, 160), ind(a("tab"), a("llv", 0, 10)))
-        cp(a("llv", 20, 40), a("lv", 20, 40))
-        rn(256, C)
-        act(a("vf"), ind(a("tab"), a("llv", 20, 40)))
+        tt(a("npr"), a("rn"), a("hh"), OP.is_equal)
+        act(a("lenr"), a("npr"), scale=float(C))
+        if t == 0:
+            act(a("cv4"), ind(a("blk", 16, 32), a("lpm")))
+        conv("cv", a("rn"), "cvs")
+        tt(a("lenb"), a("npr"), a("lenn"), OP.mult)
+        ts(a("lb"), w16("cv"), 1.0 / (M * SC), OP.mult, col(3), OP.add)
         for b in range(4):
             mm(4 + b, "qe", "se", 128 * b, "lc%d" % t, "ls%d" % t, 0, C)
         for b in range(4):
             act(a("db", b, 4 * C, 4), bank(4 + b, C))
         dma("y", T.db[:, 4 * C:8 * C], T.db[:, 0:4 * C], [a("db", 4 * C, 8 * C)], [a("db", 0, 4 * C)])
-        scan(a("tt", 2 * C + 1, 3 * C + 1), a("lenr"), a("d1"), float(CC // 2 - 1), OP.add, OP.subtract)
-        tt(a("a2"), ind(a("tt"), a("lb")), a("rn"), OP.add)
+        scan(a("tt", 2 * C + 1, 3 * C + 1), a("lenb"), a("d1"), float(CC // 2 - 1), OP.add, OP.subtract)
+        value(0, 112)
+        tt(a("a2"), ind(a("tt"), a("lb")), a("tg"), OP.add)
+        value(112, 216)
         conv("cvo", a("a2"), "cvh")
+        value(216, C)
         ts(a("lpos"), w16("cvo"), col(8), OP.add, 0.5, OP.mult)
         cp(ind(a("orow"), a("lpos")), a("vf"))
         conv("cv", a("orow", 0, 136), "cv4", 0, 136)
@@ -458,18 +453,17 @@ def rank_program(g, core, T, topo):
             tt(a("x128", 8 * A + b, 4 * C, 4), a("ps", e0 + 3 * A - C, e0 + A), a("z128", 8 * A + b, 4 * C, 4), OP.add)
         qn, sn = "qx%d" % (t + 1), "sx%d" % (t + 1)
         lq, ls = ("qv", "sv") if last else ("qu2", "su2")
-        ts(a("xb", 4 * A, 8 * A), a("x128", 4 * A, 8 * A), 0.0078125, OP.mult)
-        ts(a("xb", 8 * A, 4 * C), a("x128", 8 * A, 4 * C), 0.0078125, OP.mult)
-        for c0, c1 in ((0, 8), (8, 32)):
+        for c0, c1, r0, r1 in ((0, 8, A, 2 * A), (8, 32, 2 * A, C)):
             e0, e1 = 16 * c0, 16 * c1
             tt(a("z", e0, e1), ind(da, a(ll, c0, c1)), a("g2a", e0 + 4, e1 + 4), OP.subtract)
             act(a("z128", e0, e1), a("z", e0, e1), scale=128.0)
-        quant(qn, sn, A, C, a("xb", 4 * A, 4 * C))
-        if last:
-            dma("y", T.oc[:, 4 * A:4 * C], u8(a(qn, A, C)), [], [a(qn, A, C)])
+            rescale(r0, r1)
         quant("qz", "zs", 0, A, a("z", 0, 4 * A))
         for b in range(4):
             mm(b, "qw", "sw", 128 * b, "qz", "zs", 0, A)
+        quant(qn, sn, A, C, a("xb", 4 * A, 4 * C))
+        if last:
+            dma("y", T.oc[:, 4 * A:4 * C], u8(a(qn, A, C)), [], [a(qn, A, C)])
         mm(4, lq, ls, 0, qn, sn, A, C)
         if last:
             act(a("ys", A, C), bank(4, C - A))
@@ -478,7 +472,7 @@ def rank_program(g, core, T, topo):
             tt(a("x128", b, 4 * A, 4), bank(b, A), a("z128", b, 4 * A, 4), OP.add)
         if not last:
             defects(A, C, 4)
-        ts(a("xb", 0, 4 * A), a("x128", 0, 4 * A), 0.0078125, OP.mult)
+        rescale(0, A)
         quant(qn, sn, 0, A, a("xb", 0, 4 * A))
         mm(5, lq, ls, 0, qn, sn, 0, A)
         if last:

from concourse.mybir import dt, AluOpType, ActivationFunctionType

C, A, R = 320, 128, 3
STEP = [1, 2, 3]
M = 2048
CC = 2 * 640 * M
K = float(2 ** 22)
KH = 640.0 / K
BIG = float(2 ** 24)
SC = 2.0 ** -23
F32, BF, I32, U16, Q4, U8 = "float32", "bfloat16", "int32", "uint16", "float8_e4m3fn_x4", "uint8"
LISTS = ["lpm", "lend", "lpar", "lp1", "lrs", "ldr", "lq", "lpp", "lpost", "lsig", "lb", "lpos", "lvn"]
LQ = 20 * LISTS.index("lq")

SCRATCH = {"ps": ("psum", [128, 4096], F32)}
for _d, _l in (
    (BF, "xb:3840 db:3840 x128:1280 z:1280 z128:1280 g2o:784 g2a:528 ub:512 vb:512 ones:516 e0:516 e1:516 junk:3360 "
         "cvp m2 q p:336 ph:336 pp osg:336 pcv kk yy jp ycv jcv sg:336 mk:336 npr"),
    ("float16", "a2 cvh cvo cf lenn lenb"),
    (Q4, "qz qy:128 qu:128 qu2:128 qv:128 qw:512 qe:512 qx0 qx1 qx2 qx3 lc0 lc1 lc2"),
    (U8, "zs ys2:128 su:128 su2:128 sv:128 sw:512 se:512 sx0 sx1 sx2 sx3 ls0 ls1 ls2"),
    (I32, "szw:20 prw:20 pi:8 mi:32 mj:32"),
    (U16, "li:%d lu:8 ll0:34 ll1:34 ll2:34 lo0:96 lo1:96 lo2:96" % (20 * len(LISTS))),
    (F32, "pf:8 col:16 i16:20 ii:16 nw:20 nb:20 ba:64 blk:32 cv16 cv4 tab:648 cs:1856 c2 tt:968 "
          "s1:20 s2:20 s3:20 s4:20 s6:40 hl:60 acc:20 n1k:20 cvs endr wr r0 cv cvb hh ssw sswp pre dd:328 kw:20 "
          "vn vs cc:328 ua vbk ff gg fn gn rn d1 lenr vf tg orow ys"),
):
    for _e in _l.split():
        SCRATCH[_e.split(":")[0]] = ("sbuf", [128, int(_e.split(":")[1]) if ":" in _e else C], _d)

NDMA = 30
SEMAPHORES = (["cv", "cs", "ct", "cg", "left"] + ["qa%d" % t for t in range(R)] + ["la%d" % t for t in range(R)]
              + ["d%d" % i for i in range(NDMA)])
OP = AluOpType
AF = ActivationFunctionType


def rank_program(g, core, T, topo):
    rank = T.rank_of(core)
    if rank is None:
        return
    N = len(T.cores)
    eng = {"v": g.vector, "s": g.scalar, "t": g.tensor, "g": g, "y": g.sync}
    semof = {"v": "cv", "s": "cs", "t": "ct", "g": "cg"}
    count = {}
    known = {k: {} for k in eng}
    hist = {}
    ndma = [0]

    def a(name, lo=0, hi=None, step=1, rev=False):
        if name in LISTS:
            name, lo, hi = "li", 20 * LISTS.index(name), 20 * LISTS.index(name) + 20
        if hi is None:
            hi = SCRATCH[name][1][1]
        bits = 0
        if name == "ps":
            bits = 1 << (lo // 512)
        elif step == 1:
            bits = ((1 << (hi - lo)) - 1) << lo
        else:
            for c in range(lo, hi, step):
                bits |= 1 << c
        if rev:
            last = lo + (hi - lo - 1) // step * step
            v = T[name][:, last::-step] if lo - step < 0 else T[name][:, last:lo - step:-step]
        elif step == 1:
            v = T[name][:, lo:hi]
        else:
            v = T[name][:, lo:hi:step]
        return (v, [(name, bits)])

    def ind(win, off):
        return (win[0].indirect(off[0]), win[1] + off[1], len(win[1]))

    def wait(qn, tok):
        if known[qn].get(tok[0], 0) >= tok[1]:
            return
        eng[qn].wait_ge(T.sem[tok[0]], tok[1])
        for k2, v2 in tok[2].items():
            if known[qn].get(k2, 0) < v2:
                known[qn][k2] = v2
        known[qn][tok[0]] = tok[1]

    def run(qn, fn, outs, ins, dma=False, inc=True):
        wr, rd = [], []
        for o in outs:
            n = o[2] if len(o) > 2 else len(o[1])
            wr += o[1][:n]
            rd += o[1][n:]
        for i in ins:
            for e in i[1]:
                (wr if e[0] == "ps" else rd).append(e)
        need = {}
        for lst, both in ((wr, True), (rd, False)):
            for name, bits in lst:
                for kind, b, tok in hist.get(name, []):
                    if b & bits and (both or kind == "w"):
                        if tok[0] not in need or need[tok[0]][1] < tok[1]:
                            need[tok[0]] = tok
        for tok in sorted(need.values(), key=lambda t: -len(t[2])):
            wait(qn, tok)
        call = fn()
        if not inc:
            return
        if dma:
            s, n = "d%d" % ndma[0], 16
            ndma[0] += 1
        else:
            s, n = semof[qn], 1
        call.then_inc(T.sem[s], n)
        count[s] = count.get(s, 0) + n
        tok = (s, count[s], dict(known[qn]))
        for name, bits in wr:
            h = [[k2, b & ~bits, t2] for k2, b, t2 in hist.get(name, []) if b & ~bits]
            hist[name] = h + [["w", bits, tok]]
        for name, bits in rd:
            hist.setdefault(name, []).append(["r", bits, tok])

    def aps(*xs):
        return [x for x in xs if isinstance(x, tuple)]

    def val(x):
        return x[0] if isinstance(x, tuple) else x

    def ts(o, i, s1, op0, s2=None, op1=None):
        if op1 is None:
            run("v", lambda: g.vector.tensor_scalar(o[0], i[0], val(s1), None, op0), [o], aps(i, s1))
        else:
            run("v", lambda: g.vector.tensor_scalar(o[0], i[0], val(s1), val(s2), op0, op1), [o], aps(i, s1, s2))

    def tt(o, i0, i1, op):
        run("v", lambda: g.vector.tensor_tensor(o[0], i0[0], i1[0], op), [o], [i0, i1])

    def cp(o, i):
        run("v", lambda: g.vector.tensor_copy(o[0], i[0]), [o], [i])

    def ms(o, c):
        run("v", lambda: g.vector.memset(o[0], c), [o], [])

    def scan(o, d0, d1, init, op0, op1):
        run("v", lambda: g.vector.tensor_tensor_scan(o[0], d0[0], d1[0], val(init), op0, op1), [o], aps(d0, d1, init))

    def act(o, i, f=None, bias=None, scale=None, acc=None):
        kw = {}
        if bias is not None:
            kw["bias"] = val(bias)
        if scale is not None:
            kw["scale"] = scale
        if acc is not None:
            kw["accum_out"] = acc[0]
        if f is None:
            f = AF.Copy if bias is None else AF.Identity
        run("s", lambda: g.scalar.activation(o[0], i[0], f, **kw), aps(o, acc), aps(i, bias))

    def quant(qn, sn, lo, hi, src):
        o, s = a(qn, lo, hi), a(sn, lo, hi)
        run("v", lambda: g.vector.quantize_mx(o[0], s[0], src[0]), [o, s], [src])

    def mm(bank, lq, ls, llo, rq, rs, lo, hi):
        o = a("ps", 512 * bank, 512 * bank + hi - lo)
        x = [a(lq, llo, llo + 128), a(ls, llo, llo + 128), a(rq, lo, hi), a(rs, lo, hi)]
        run("t", lambda: g.tensor.matmul_mx(o[0], x[0][0], x[1][0], x[2][0], x[3][0], True, True), [o], x)

    def iota(o, pat, base, cm, small=True):
        if small:
            run("g", lambda: g.iota(o[0], pat, base, cm, allow_small_or_imprecise_dtypes=True), [o], [])
        else:
            run("g", lambda: g.iota(o[0], pat, base, cm), [o], [])

    def dma(qn, out, in_, outs, ins):
        run(qn, lambda: eng[qn].dma_start(out, in_), outs, ins, dma=True)

    def u8(x):
        return x[0].bitcast(dt.uint8)

    def send(t, src, dst, sem):
        to = T.cores[(rank + STEP[t]) % N]
        rid, pid, _ = topo.addr(to)
        m = topo.mask(core, to)
        run("g", lambda: g.remote_dma(dst, src[0], T.sem[sem], T.sem.left, pid, rid, m), [], [src], inc=False)
        count["left"] = count.get("left", 0) + len(topo.engines(core, to))

    def conv(o, row, table="cv16", lo=0, hi=C):
        scan(a(o, lo, hi), a(table, lo, hi), row, 0.0, OP.add, OP.max)

    def w16(name):
        return a(name, 15, C, 16)

    def col(i):
        return a("col", i, i + 1)

    def bank(b, n):
        return a("ps", 512 * b, 512 * b + n)

    for t in range(R):
        frm = T.cores[(rank - STEP[t]) % N]
        ne = len(topo.engines(frm, core))
        count["qa%d" % t] = 2 * ne
        count["la%d" % t] = ne
        for nm in ("lc%d" % t, "ls%d" % t):
            hist[nm] = [["w", a(nm)[1][0][1], ("qa%d" % t, 2 * ne, {})]]
        hist["ll%d" % t] = [["w", a("ll%d" % t)[1][0][1], ("la%d" % t, ne, {})]]

    dma("y", T.szw[:], T.sz[:], [a("szw")], [])
    dma("s", T.prw[:], T.pr[:], [a("prw")], [])
    dma("y", T.ub[:], T.u[:], [a("ub")], [])
    dma("s", T.xb[:, 0:4 * C], T.x[:], [a("xb", 0, 4 * C)], [])
    dma("y", T.xb[:, 4 * C:8 * C], T.x[:], [a("xb", 4 * C, 8 * C)], [a("xb", 0, 4)])
    dma("y", u8(a("qw")), T.wc[:], [a("qw")], [])
    dma("y", T.sw[:], T.ws[:], [a("sw")], [])
    dma("y", T.vb[:], T.v[:], [a("vb")], [])

    ip, endw, n1k, osg = a("pi", 4, 5), a("hl", 40, 60), a("n1k"), a("osg", 0, C)
    iota(ip, [[0, 1]], 0, 1, small=False)
    iota(a("i16"), [[16, 20]], 0, 0)
    iota(a("ii"), [[1, 16]], 16, 0)
    iota(a("tab"), [[1, 648]], 0, 0)
    iota(a("ones"), [[0, 516]], 1, 0)
    for k in range(2):
        o = a("e%d" % k)
        run("g", lambda: g.affine_select(o[0], T.ones[:], [[1, 516]], OP.is_equal, 0.0, -2 - k, -4), [o], [a("ones")])
    ms(a("m2"), -2.0)
    ms(a("p", 0, 1), 2.0)
    ms(a("ph", 0, 1), 0.5)
    ms(a("dd", 0, 1), 0.0)
    ms(a("sg", C, C + 1), -1.0)
    ms(a("osg", C, C + 1), 1.0)
    ms(a("mk", C, C + 1), 0.0)
    ms(a("cc", C, C + 1), 1.0)
    ms(a("g2o", 768, 784), 0.0)
    ts(a("pi", 0, 1), ip, 15, OP.bitwise_and)
    ts(a("pi", 1, 2), ip, 2, OP.arith_shift_right, 3, OP.bitwise_and)
    ts(a("pi", 2, 3), ip, 3, OP.bitwise_and)
    cp(a("lu"), a("i16", 0, 8))
    cp(a("pf", 0, 3), a("pi", 0, 3))
    ts(a("nw"), a("i16"), a("pf", 0, 1), OP.add)
    ts(a("mi", 0, 16), a("ii"), a("pf", 0, 1), OP.subtract)
    ts(a("mi", 16, 32), a("ii"), a("pf", 1, 2), OP.subtract)
    ts(a("lpm"), a("i16"), 0.0, OP.mult, a("pf", 0, 1), OP.add)
    ts(a("nb"), a("i16"), a("pf", 0, 1), OP.add, -1.0, OP.mult)
    ts(a("pf", 4, 5), a("pf", 0, 1), 15.0, OP.is_lt, K, OP.mult)
    ts(a("pf", 5, 6), a("pf", 1, 2), 3.0, OP.is_lt, -4 * K, OP.mult)
    ts(a("mj", 0, 16), a("mi", 0, 16), 15, OP.bitwise_and)
    ts(a("mj", 16, 32), a("mi", 16, 32), 3, OP.bitwise_and)
    ts(a("nb"), a("nb"), -0.5, OP.add)
    ts(a("hl", 0, 20), a("i16"), 16.0, OP.add)
    kf = a("pf", 4, 5)
    tt(endw, a("nw"), a("szw"), OP.add)
    ts(a("ba", 0, 32), a("mj"), 0.0, OP.is_equal, -BIG, OP.mult)
    ts(a("ba", 32, 64), a("mj"), 1.0, OP.is_equal, K, OP.mult)
    ts(col(0), kf, -1.0, OP.mult)
    cp(a("lend"), endw)
    tt(a("s1"), a("nw"), a("prw"), OP.subtract)
    tt(a("blk"), a("ba", 0, 32), a("ba", 32, 64), OP.add)
    cp(a("lpar"), a("prw"))
    cp(a("endr"), ind(a("tab"), a("lend")))
    off = 0
    for c in range(19, -1, -1):
        n = 16 * c + 16
        act(a("junk", off, off + n), a("endr", 0, n), AF.Sign, bias=a("nb", c, c + 1), acc=a("acc", c, c + 1))
        off += n
    act(a("cv16"), ind(a("blk", 0, 16), a("lpm")))
    act(a("cvp"), a("cv16"), scale=4.0 / K)
    act(a("cvh"), a("cv16"), scale=KH)
    for e, n, f in ((0, 512, -0.5), (512, 512, -0.5), (1024, 512, 0.5), (1536, C, 1.0)):
        act(a("cs", e, e + n), a("tab", 0, n), bias=f * (2 - CC) * SC, scale=f * 2 * M * SC)
    ts(a("s2"), a("s1"), 1.0, OP.is_gt)
    tt(a("s4"), a("s1"), endw, OP.add)
    quant("qu", "su", 0, 128, a("ub"))
    ts(a("ldr"), a("s4"), -1.0, OP.add)
    ts(a("lp1"), a("prw"), 1.0, OP.add)
    tt(a("s3"), a("s2"), a("szw"), OP.mult)
    lu = a("lu")
    run("v", lambda: g.vector.tensor_copy(T.qu2[:, 0:128].bitcast(dt.uint32),
                                          T.qu[:, 0:128].bitcast(dt.uint32).indirect(lu[0])),
        [a("qu2")], [a("qu"), lu])
    run("v", lambda: g.vector.tensor_copy(T.su2[:, 0:128], T.su[:, 0:128].indirect(lu[0])), [a("su2")], [a("su"), lu])
    tt(a("s4"), endw, a("s3"), OP.subtract)
    quant("qx0", "sx0", 0, C, a("xb", 0, 4 * C))
    cp(a("lrs"), a("s4"))

    def spread(t):
        send(t, (u8(a("qx%d" % t)), a("qx%d" % t)[1]), u8(a("lc%d" % t)), "qa%d" % t)
        send(t, a("sx%d" % t), a("ls%d" % t)[0], "qa%d" % t)

    def defects(lo, hi, b):
        ts(a("q", lo, hi), bank(b, hi - lo), 0.0, OP.is_gt, 0.5, OP.subtract)

    def unit(t, b):
        if t == 0:
            s = 2 - 2 * (b // 2)
            quant("qe", "se", 128 * b, 128 * b + 128, a("e%d" % (b % 2), s, s + 512))

    def value(lo, hi):
        tt(a("vf", lo, hi), a("lenr", lo, hi), a("tab", lo, hi), OP.add)

    def rescale(lo, hi):
        ts(a("xb", 4 * lo, 4 * hi), a("x128", 4 * lo, 4 * hi), 0.0078125, OP.mult)

    mm(0, "qu2", "su2", 0, "qx0", "sx0", 0, C)
    spread(0)
    ts(a("s6", 0, 20), a("szw"), 2.0, OP.mult, -2.0, OP.add)
    cp(a("r0"), ind(a("tab"), a("ldr")))
    tt(a("hl", 20, 40), a("hl", 0, 20), a("s6", 0, 20), OP.add)
    defects(0, C, 0)
    iota(a("c2"), [[0, C]], M * 2 - 1, 0)
    iota(a("tt"), [[0, 968]], CC // 2 - 1, 0)
    iota(a("db", 8 * C, 12 * C), [[0, 4 * C]], 0, 0)
    dma("y", T.xb[:, 8 * C:12 * C], T.db[:, 8 * C:12 * C], [a("xb", 8 * C, 12 * C)], [a("db", 8 * C, 12 * C)])

    for t in range(R):
        lo, ll = "lo%d" % t, "ll%d" % t
        last = t == R - 1
        P = a("ph", 0, C)
        scan(a("ph", 1, C + 1), a("q"), a("m2"), 0.5, OP.mult, OP.mult)
        scan(a("p", 1, C + 1), a("q"), a("m2"), 2.0, OP.mult, OP.mult)
        pw = a("ph", 0, C + 1)
        if t:
            act(a("pp"), ind(pw, a("lpost")))
        else:
            tt(a("wr"), ind(a("endr"), a("lpar")), a("r0"), OP.subtract)
        tt(a("kk"), a("q"), P, OP.min)
        tt(osg, ind(pw, a("lend")), a("p", 0, C), OP.mult)
        if t == 0:
            tt(a("s6", 0, 20), a("hl", 0, 20), a("acc"), OP.subtract)
            tt(a("s6", 20, 40), a("hl", 20, 40), a("acc"), OP.subtract)
            tt(a("yy"), a("kk"), osg, OP.add)
            ts(a("li", LQ, LQ + 40), a("s6"), 0.5, OP.mult)
            act(a("jp"), ind(a("yy"), a("lpar")), bias=-1.0)
            ts(col(1), kf, KH, OP.mult, (C - 1) / 2.0, OP.add)
            ts(col(2), kf, -4.0 / K, OP.mult)
            ts(col(3), kf, -1.0 / M, OP.mult, float(CC // M), OP.add)
            ts(col(5), kf, 4.0 / K, OP.mult, 1.0, OP.add)
            cp(ind(a("r0"), a("lpp")), a("tab", 0, C))
            tt(a("hh"), ind(pw, a("lp1")), a("wr"), OP.mult)
            conv("cv", a("r0"))
            tt(a("ssw"), ind(a("osg", 0, C + 1), a("lrs")), a("hh"), OP.mult)
            ts(a("lpost"), w16("cv"), col(0), OP.add)
            conv("ycv", a("yy"), "cvp")
            conv("pcv", P, "cvp")
            act(a("sswp"), ind(a("ssw"), a("lpost")))
            cp(a("pp"), ind(pw, a("lpost")))
            scan(a("pre"), a("ssw"), P, 0.0, OP.add, OP.subtract)
            scan(a("dd", 1, C + 1), a("sswp"), a("pp"), 0.0, OP.add, OP.subtract)
            ts(a("s2"), w16("ycv"), 1.0, OP.add, col(5), OP.min)
            conv("jcv", a("jp"), "cvp")
            ts(a("kw"), w16("pcv"), col(2), OP.add)
            ts(col(6), kf, -4096.0 / K, OP.mult, 512.0, OP.add)
            ts(n1k, a("nw"), 1.0 / 1024, OP.mult)
        else:
            tt(a("hh"), ind(pw, a("lp1")), a("wr"), OP.mult)
            tt(a("yy"), a("kk"), osg, OP.add)
            act(a("jp"), ind(a("yy"), a("lpar")), bias=-1.0)
            tt(a("ssw"), ind(a("osg", 0, C + 1), a("lrs")), a("hh"), OP.mult)
            act(a("sswp"), ind(a("ssw"), a("lpost")))
            conv("ycv", a("yy"), "cvp")
            conv("pcv", P, "cvp")
            scan(a("pre"), a("ssw"), P, 0.0, OP.add, OP.subtract)
            ts(a("s2"), w16("ycv"), 1.0, OP.add, col(5), OP.min)
            conv("jcv", a("jp"), "cvp")
            ts(a("kw"), w16("pcv"), col(2), OP.add)
            scan(a("dd", 1, C + 1), a("sswp"), a("pp"), 0.0, OP.add, OP.subtract)
        tt(a("s3"), a("s2"), w16("jcv"), OP.max)
        tt(a("kw"), a("kw"), a("szw"), OP.mult)
        tt(a("a2", 0, 160), ind(a("dd", 0, C + 1), a("li", LQ, LQ + 10)), a("pre", 0, 160), OP.subtract)
        tt(a("s4"), a("s3"), n1k, OP.add)
        tt(a("a2", 160, C), ind(a("dd", 0, C + 1), a("li", LQ + 10, LQ + 20)), a("pre", 160, C), OP.subtract)
        ts(a("lvn"), a("s4"), 1024.0, OP.mult, col(6), OP.add)
        if t == 0:
            ts(col(8), kf, -KH, OP.mult)
            tt(col(4), a("pf", 5, 6), a("pf", 2, 3), OP.add)
        conv("cvo", a("a2"), "cvh")
        act(a("vn"), ind(a("cs"), a("lvn")))
        act(a("sswp"), a("vn"), AF.Abs)
        act(a("hh"), a("sswp"), scale=-1.0)
        unit(t, 0)
        tt(a("s1"), a("kw"), w16("cvo"), OP.subtract)
        unit(t, 1)
        ts(a("lsig"), a("s1"), col(1), OP.add)
        unit(t, 2)
        cp(ind(a("vs"), a("lsig")), a("vn"))
        unit(t, 3)
        act(a("ua"), a("vs"), AF.Abs)
        act(a("sg", 0, C), a("vs"), AF.Sign)
        ts(a("cc", 0, C), a("vs"), 0.0, OP.is_lt, 2 * SC, OP.max)
        scan(a("ff"), a("cc", 0, C), a("vs"), 1.0, OP.add, OP.min)
        act(a("mk", 0, C), a("sg", 0, C), AF.Relu)
        act(a("fn"), ind(a("ff"), a("lsig")))
        if t == 0:
            act(a("cvs"), a("cv16"), scale=SC)
        tt(a("vbk"), a("ua"), a("sg", 1, C + 1), OP.mult)
        scan(a("cf"), a("mk", 0, C), a("ones", 0, C), 0.0, OP.mult, OP.add)
        scan(a("gg", rev=True), a("cc", 1, C + 1, rev=True), a("vbk", rev=True), 1.0, OP.add, OP.min)
        scan(a("gn", rev=True), a("mk", 1, C + 1, rev=True), a("cf", rev=True), 0.0, OP.mult, OP.max)
        act(a("lenn"), ind(a("gn"), a("lsig")), scale=2.0)
        tt(a("rn"), ind(a("gg"), a("lsig")), a("fn"), OP.min)
        act(a("d1"), osg, bias=float(M + 1))
        act(a("tg"), a("rn"), scale=1 / SC)
        scan(a("tt", 0, 2 * C, 2, rev=True), a("c2"), a("osg", 0, C, rev=True), float(2 * C - 2 * M * C - 2 + CC),
             OP.add, OP.subtract)
        tt(a("npr"), a("rn"), a("hh"), OP.is_equal)
        act(a("lenr"), a("npr"), scale=float(C))
        if t == 0:
            act(a("cv4"), ind(a("blk", 16, 32), a("lpm")))
        conv("cv", a("rn"), "cvs")
        tt(a("lenb"), a("npr"), a("lenn"), OP.mult)
        ts(a("lb"), w16("cv"), 1.0 / (M * SC), OP.mult, col(3), OP.add)
        for b in range(4):
            mm(4 + b, "qe", "se", 128 * b, "lc%d" % t, "ls%d" % t, 0, C)
        for b in range(4):
            act(a("db", b, 4 * C, 4), bank(4 + b, C))
        dma("y", T.db[:, 4 * C:8 * C], T.db[:, 0:4 * C], [a("db", 4 * C, 8 * C)], [a("db", 0, 4 * C)])
        scan(a("tt", 2 * C + 1, 3 * C + 1), a("lenb"), a("d1"), float(CC // 2 - 1), OP.add, OP.subtract)
        value(0, 112)
        tt(a("a2"), ind(a("tt"), a("lb")), a("tg"), OP.add)
        value(112, 216)
        conv("cvo", a("a2"), "cvh")
        value(216, C)
        ts(a("lpos"), w16("cvo"), col(8), OP.add, 0.5, OP.mult)
        cp(ind(a("orow"), a("lpos")), a("vf"))
        conv("cv", a("orow", 0, 136), "cv4", 0, 136)
        conv("cvb", a("orow", A, C), "cv4", A, C)
        ts(a(lo, 0, 34), a("cv", 3, 136, 4), 4.0, OP.mult, col(4), OP.add)
        send(t, a(lo, 0, 34), a(ll)[0], "la%d" % t)
        ts(a(lo, 48, 96), a("cvb", A + 3, C, 4), 4.0, OP.mult, col(4), OP.add)
        if last:
            ts(a("tg"), a("orow"), float(C), OP.is_ge, -float(C), OP.mult)
        if t == 0:
            quant("qv", "sv", 0, 128, a("vb"))
        wa, wb = a("xb", 0, 8 * C), a("xb", 4 * C, 12 * C)
        for c0, c1 in ((0, 12), (12, 34), (34, 48)):
            act(a("g2o", 16 * c0, 16 * c1), ind(wb, a(lo, 48 + c0, 48 + c1)))
        for c0, c1 in ((0, 10), (10, 32), (32, 48)):
            e0, e1 = 4 * A + 16 * c0, 4 * A + 16 * c1
            tt(a("z", e0, e1), ind(wa, a(lo, 48 + c0, 48 + c1)), a("g2o", 16 * c0 + 4, 16 * c1 + 4), OP.subtract)
            act(a("z128", e0, e1), a("z", e0, e1), scale=128.0)
        quant("qz", "zs", A, 2 * A, a("z", 4 * A, 8 * A))
        quant("qy", "ys2", 0, A, a("z", 4 * (C - A), 4 * C))
        for b in range(4):
            mm(b, "qw", "sw", 128 * b, "qz", "zs", A, 2 * A)
        for b in range(4):
            mm(4 + b, "qw", "sw", 128 * b, "qy", "ys2", 0, A)
        if last:
            tt(a("lenr"), a("tg"), a("orow"), OP.add)
            dma("y", T.ot[:], T.lenr[0:128:16, :], [], [a("lenr")])
        da, dbb = a("db", 0, 8 * C), a("db", 4 * C, 12 * C)
        for c0, c1 in ((0, 10), (10, 33)):
            act(a("g2a", 16 * c0, 16 * c1), ind(dbb, a(ll, c0, c1)))
        for b in range(4):
            tt(a("x128", 4 * A + b, 8 * A, 4), bank(b, A), a("z128", 4 * A + b, 8 * A, 4), OP.add)
        for b in range(4):
            e0 = 512 * (4 + b)
            tt(a("x128", 8 * A + b, 4 * C, 4), a("ps", e0 + 3 * A - C, e0 + A), a("z128", 8 * A + b, 4 * C, 4), OP.add)
        qn, sn = "qx%d" % (t + 1), "sx%d" % (t + 1)
        lq, ls = ("qv", "sv") if last else ("qu2", "su2")
        for c0, c1, r0, r1 in ((0, 8, A, 2 * A), (8, 32, 2 * A, C)):
            e0, e1 = 16 * c0, 16 * c1
            tt(a("z", e0, e1), ind(da, a(ll, c0, c1)), a("g2a", e0 + 4, e1 + 4), OP.subtract)
            act(a("z128", e0, e1), a("z", e0, e1), scale=128.0)
            rescale(r0, r1)
        quant("qz", "zs", 0, A, a("z", 0, 4 * A))
        for b in range(4):
            mm(b, "qw", "sw", 128 * b, "qz", "zs", 0, A)
        quant(qn, sn, A, C, a("xb", 4 * A, 4 * C))
        if last:
            dma("y", T.oc[:, 4 * A:4 * C], u8(a(qn, A, C)), [], [a(qn, A, C)])
        mm(4, lq, ls, 0, qn, sn, A, C)
        if last:
            act(a("ys", A, C), bank(4, C - A))
            dma("s", T.y[:, A:C], T.ys[:, A:C], [], [a("ys", A, C)])
        for b in range(4):
            tt(a("x128", b, 4 * A, 4), bank(b, A), a("z128", b, 4 * A, 4), OP.add)
        if not last:
            defects(A, C, 4)
        rescale(0, A)
        quant(qn, sn, 0, A, a("xb", 0, 4 * A))
        mm(5, lq, ls, 0, qn, sn, 0, A)
        if last:
            cp(a("ys", 0, A), bank(5, A))
            dma("y", T.oc[:, 0:4 * A], u8(a(qn, 0, A)), [], [a(qn, 0, A)])
            for k in range(4):
                dma("ys"[k % 2], T.osc[4 * k:4 * k + 4, :], T[sn][32 * k:32 * k + 4, :], [], [a(sn)])
            dma("s", T.y[:, 0:A], T.ys[:, 0:A], [], [a("ys", 0, A)])
        else:
            spread(t + 1)
            dma("y", T.xb[:, 4 * C:8 * C], T.xb[:, 0:4 * C], [a("xb", 4 * C, 8 * C)], [a("xb", 0, 4 * C)])
            defects(0, A, 5)

    for s, n in count.items():
        g.wait_ge(T.sem[s], n)
